import numpy as np
import ml_dtypes


def mxq(x, axis, fmt="e4m3"):
    dtype, down = {"e4m3": (ml_dtypes.float8_e4m3fn, 7), "e5m2": (ml_dtypes.float8_e5m2, 14)}[fmt]
    v = np.moveaxis(np.asarray(x, np.float32).astype(ml_dtypes.bfloat16).astype(np.float64), axis, -1)
    blocks = v.reshape(v.shape[:-1] + (-1, 32))
    amax = np.abs(blocks).max(-1, keepdims=True)
    byte = np.maximum(np.where(amax > 0, np.frexp(amax)[1] - 1 + 127, 0) - down, 1)
    scale = np.exp2(byte - 127.0)
    codes = (blocks / scale).astype(np.float32).astype(dtype).astype(np.float64)
    return np.moveaxis((codes * scale).reshape(v.shape), -1, axis)


WIDE = False


def mx_kscale(k):
    if not WIDE:
        return np.ones(k)
    levels = np.array([24, -24, 12, -12, 0])
    if k % 512:
        return np.exp2(np.random.permutation(np.resize(levels, k // 32))).repeat(32)
    a = np.empty((k // 512, 16))
    for p in range(k // 512):
        a[p, :8] = np.random.permutation(np.resize(levels, 8))
        for g in range(8):
            far = levels[np.abs(levels - a[p, g]) >= 10]
            a[p, g + 8] = far[np.random.randint(len(far))]
    return np.exp2(a.ravel()).repeat(32)


def f64(x):
    return np.asarray(x).astype(np.float64)


def striped(idx):
    return np.tile(idx.reshape(-1, 16).T, (8, 1)).astype(np.uint16)


def unstriped(offs):
    return offs[:16].T.reshape(-1).astype(np.int64)


E2M1 = np.array([0.0, 0.5, 1.0, 1.5, 2.0, 3.0, 4.0, 6.0, -0.0, -0.5, -1.0, -1.5, -2.0, -3.0, -4.0, -6.0])


def pack_weight(w, fmt):
    k, n = w.shape
    w = f64(np.asarray(w, np.float32).astype(ml_dtypes.bfloat16)).reshape(k // 32, 32, n)
    amax = np.abs(w).max(1)
    if fmt == "e4m3":
        byte = np.frexp(amax)[1] - 1 + 127 - 7
    else:
        mant, ex = np.frexp(amax / 6.0)
        byte = np.where(mant > 0.5, ex, ex - 1) + 127
    byte = np.clip(np.where(amax > 0, byte, 1), 1, 254)
    scaled = (w * np.exp2(127.0 - byte)[:, None, :]).reshape(k, n).astype(np.float32)
    by_word = np.ascontiguousarray(scaled.reshape(k // 512, 128, 4, n).transpose(0, 1, 3, 2))
    if fmt == "e4m3":
        words = by_word.astype(ml_dtypes.float8_e4m3fn).view(np.uint8)
    else:
        c = by_word.astype(ml_dtypes.float4_e2m1fn).view(np.uint8) & 0xF
        words = (c[..., 0::2] | (c[..., 1::2] << 4)).reshape(k // 512, 128, 2 * n)
    return np.ascontiguousarray(words), np.ascontiguousarray(byte.astype(np.uint8).reshape(k // 512, 16, n))


def unpack_weight(words, scales, fmt):
    g, _, n = scales.shape
    words = np.ascontiguousarray(words).reshape(g, 128, n, -1)
    if fmt == "e4m3":
        vals = words.view(ml_dtypes.float8_e4m3fn).astype(np.float64)
    else:
        nib = np.empty((g, 128, n, 4), np.uint8)
        nib[..., 0::2] = words & 0xF
        nib[..., 1::2] = words >> 4
        vals = E2M1[nib]
    vals = vals * np.repeat(np.exp2(scales.astype(np.float64) - 127.0), 8, axis=1)[..., None]
    return vals.transpose(0, 1, 3, 2).reshape(g * 512, n)


def pack_table4(v):
    words, scales = pack_weight(v, "e2m1")
    g, t = words.shape[0] // 2, v.shape[1]
    return np.ascontiguousarray(words.reshape(g, 2, 128, t, 2).transpose(0, 2, 3, 1, 4).reshape(g, 128, t, 4)), scales


def unpack_table4(words, scales):
    g, _, t, _ = words.shape
    return unpack_weight(words.reshape(g, 128, t, 2, 2).transpose(0, 3, 1, 2, 4).reshape(2 * g, 128, 2 * t), scales, "e2m1")


def sigm(f):
    return 1.0 / (1.0 + np.exp(-np.maximum(f, -700.0)))


K, M, N, T, J = 1024, 1024, 1024, 2048, 1024


def setup_inputs():
    n = np.random.standard_normal
    s = mx_kscale(K)[:, None]
    s2 = mx_kscale(M)[:, None]
    h = np.tanh(n((N, T)))
    p_tab = pack_table4(h * s2)
    p_uz = pack_weight(n((M, N)) / np.sqrt(M) / s2, "e4m3")
    p_un = pack_weight(n((M, N)) / np.sqrt(M) / s2, "e4m3")
    return {
        "x": (n((K, J)) * s).astype(np.float32),
        "tab_words": p_tab[0],
        "tab_scales": p_tab[1],
        "wz": (n((K, N)) / np.sqrt(K) / s).astype(np.float32),
        "uz_words": p_uz[0],
        "uz_scales": p_uz[1],
        "wn": (n((K, N)) / np.sqrt(K) / s).astype(np.float32),
        "un_words": p_un[0],
        "un_scales": p_un[1],
        "bz": (0.3 * n(N)).astype(np.float32),
        "bn": (0.3 * n(N)).astype(np.float32),
        "hT": (h).astype(np.float32),
        "wgo": np.tile(np.random.uniform(0.5, 2.0, J), (128, 1)).astype(np.float32),
        "offs": striped(np.random.permutation(T)[:J]),
    }


def reference(x, tab_words, tab_scales, wz, uz_words, uz_scales, wn, un_words, un_scales, bz, bn, hT, wgo, offs):
    idx = unstriped(offs)
    x_ = mxq(f64(x), 0, "e4m3")
    tab_ = unpack_table4(tab_words, tab_scales)[:, idx]
    wz_ = mxq(f64(wz), 0, "e4m3")
    uz_ = unpack_weight(uz_words, uz_scales, "e4m3")
    wn_ = mxq(f64(wn), 0, "e4m3")
    un_ = unpack_weight(un_words, un_scales, "e4m3")
    sz = wz_.T @ x_ + uz_.T @ tab_
    z = sigm(sz + f64(bz)[:, None])
    sn = wn_.T @ x_ + un_.T @ tab_
    cd = np.tanh(sn + f64(bn)[:, None])
    out = np.zeros((N, T))
    out[:, idx] = f64(wgo)[0] * (f64(hT)[:, idx] + z * (cd - f64(hT)[:, idx]))
    return out

@@ -1,0 +1,278 @@
+from contextlib import ExitStack
+
+import concourse.mybir as mybir
+
+K, M, N, T, J = 1024, 1024, 1024, 2048, 1024
+FLOPS = 2 * 2 * (K + M) * N * J
+
+F32 = mybir.dt.float32
+BF16 = mybir.dt.bfloat16
+I32 = mybir.dt.int32
+U32 = mybir.dt.uint32
+U16 = mybir.dt.uint16
+U8 = mybir.dt.uint8
+FP8X4 = mybir.dt.float8_e4m3fn_x4
+FP4X4 = mybir.dt.float4_e2m1fn_x4
+ACT = mybir.ActivationFunctionType
+ALU = mybir.AluOpType
+
+P = 128
+PACK = 4
+KP = P * PACK
+PASSES = 2
+HALF = 512
+TILES = N // P
+CHUNKS = [(0, 128), (128, 128), (256, 256), (512, 256), (768, 256)]
+
+
+def tile_list_tgn_ema_kernel(
+    tc, x, tab_words, tab_scales, wz, uz_words, uz_scales, wn, un_words, un_scales, bz, bn, hT, wgo, offs, out
+):
+    nc = tc.nc
+    with ExitStack() as ctx:
+        keep = ctx.enter_context(tc.tile_pool(name="keep", bufs=1))
+        ring = ctx.enter_context(tc.tile_pool(name="ring", bufs=2))
+        psum = ctx.enter_context(tc.psum_pool(name="psum", bufs=4))
+
+        offsets = keep.tile([P, J // 16], U16, name="offsets")
+        nc.sync.dma_start(offsets[:], offs)
+
+        def listed(j0, width):
+            return offsets[:, j0 // 16 : (j0 + width) // 16]
+
+        def load_scale_rows(queue, plane, scales):
+            nc.vector.memset(plane[:], 0)
+            rows = scales.bitcast(I32)
+            for q in range(4):
+                queue.dma_start(
+                    out=plane[32 * q : 32 * q + 4, :, :], in_=rows[:, 4 * q : 4 * q + 4, :].rearrange("a r n -> r a n")
+                )
+
+        warm = keep.tile([P, 8], F32, name="warm")
+        nc.vector.memset(warm[:, 0:4], 0.0)
+        nc.scalar.activation(warm[:, 4:8], warm[:, 0:4], ACT.Sigmoid)
+
+        tab_sc = keep.tile([P, PASSES, T // 4], I32, name="tab_sc", align_bytes=64)
+        load_scale_rows(nc.sync, tab_sc, tab_scales)
+        u_sc = []
+        for name, scales in (("uz_sc", uz_scales), ("un_sc", un_scales)):
+            plane = keep.tile([P, PASSES, N // 4], I32, name=name, align_bytes=64)
+            load_scale_rows(nc.scalar, plane, scales)
+            u_sc.append(plane)
+        bias = []
+        for name, vec in (("bz_sb", bz), ("bn_sb", bn)):
+            col = keep.tile([P, TILES], F32, name=name)
+            with nc.allow_non_contiguous_dma(reason="one bias value a partition"):
+                nc.scalar.dma_start(out=col[:], in_=vec.rearrange("(c p) -> p c", p=P))
+            bias.append(col)
+        neg_bz = keep.tile([P, TILES], F32, name="neg_bz")
+        nc.vector.tensor_scalar(neg_bz[:], bias[0][:], -1.0, None, ALU.mult)
+
+        windows = []
+        for b in range(2):
+            win = keep.tile([P, T], F32, name=f"window{b}")
+            nc.gpsimd.memset(win[:], 0.0)
+            windows.append(win)
+
+        tab_w = keep.tile([P, T], I32, name="tab_w")
+        nc.sync.dma_start(out=tab_w[:], in_=tab_words[0].rearrange("p t b -> p (t b)").bitcast(I32))
+
+        v_codes, v_sc = [], []
+
+        def gather_table(h):
+            sc = keep.tile([P, PASSES, HALF], U8, name=f"v_sc{h}", align_bytes=64)
+            for a in range(PASSES):
+                nc.vector.tensor_copy(sc[:, a, :], tab_sc[:, a, :].bitcast(U8).indirect(listed(h * HALF, HALF)))
+            pairs = keep.tile([P, HALF], U32, name=f"v_pairs{h}", align_bytes=64)
+            nc.vector.tensor_copy(pairs[:], tab_w[:].bitcast(U32).indirect(listed(h * HALF, HALF)))
+            codes = keep.tile([P, PASSES * 2 * HALF], U8, name=f"v_codes{h}", align_bytes=64)
+            nc.vector.tensor_copy(
+                codes[:].bitcast(U16).rearrange("p (a j) -> p a j", a=PASSES),
+                pairs[:].bitcast(U16).rearrange("p (j a) -> p a j", a=PASSES),
+            )
+            v_codes.append(codes)
+            v_sc.append(sc)
+
+        def load_rows(raw, rows):
+            nc.sync.dma_start(out=raw, in_=rows.rearrange("(p i) w -> p i w", i=PACK))
+
+        def interleave(grouped, raw):
+            nc.scalar.copy(
+                out=grouped.rearrange("p (c e) i -> p c i e", e=4), in_=raw.rearrange("p i (c e) -> p c i e", e=4)
+            )
+
+        x_codes = keep.tile([P, PASSES, J], U32, name="x_codes", align_bytes=64)
+        x_sc = keep.tile([P, PASSES, J], U8, name="x_sc", align_bytes=64)
+
+        def load_x(a, h):
+            raw = ring.tile([P, PACK, HALF], F32, name="x_raw", tag="raw", bufs=5)
+            load_rows(raw[:], x[a * KP : (a + 1) * KP, h * HALF : (h + 1) * HALF])
+            return raw
+
+        def prep_x(a, h, raw):
+            grouped = ring.tile([P, HALF, PACK], BF16, name="x_grouped", tag="grouped", bufs=4, align_bytes=64)
+            interleave(grouped[:], raw[:])
+            cols = slice(h * HALF, (h + 1) * HALF)
+            nc.vector.quantize_mx(
+                out=x_codes[:, a, cols].bitcast(FP8X4), scales=x_sc[:, a, cols], in_=grouped[:].rearrange("p w i -> p (w i)")
+            )
+
+        w_dram = (wz, wn)
+        u_dram = (uz_words, un_words)
+        u_codes = [keep.tile([P, PASSES, N], I32, name=f"u_codes{g}", align_bytes=64) for g in range(2)]
+        w_codes, w_sc = {}, {}
+
+        def load_w(ch, g):
+            n0, width = CHUNKS[ch]
+            raw = ring.tile([P, PASSES, PACK, width], F32, name="w_raw", tag="raw", bufs=5)
+            for a in range(PASSES):
+                load_rows(raw[:, a, :, :], w_dram[g][a * KP : (a + 1) * KP, n0 : n0 + width])
+            return raw
+
+        def load_u(n0, width):
+            for g in range(2):
+                words = u_dram[g].rearrange("a p n i -> p a (n i)")[:, :, 4 * n0 : 4 * (n0 + width)].bitcast(I32)
+                nc.sync.dma_start(out=u_codes[g][:, :, n0 : n0 + width], in_=words)
+
+        def prep_w(ch, g, raw):
+            width = CHUNKS[ch][1]
+            grouped = ring.tile([P, PASSES, width, PACK], BF16, name="w_grouped", tag="grouped", bufs=4, align_bytes=64)
+            for a in range(PASSES):
+                interleave(grouped[:, a, :, :], raw[:, a, :, :])
+            codes = keep.tile([P, PASSES * width], U32, name=f"w_codes{ch}_{g}", align_bytes=64)
+            sc = keep.tile([P, PASSES * width], U8, name=f"w_sc{ch}_{g}", align_bytes=64)
+            nc.vector.quantize_mx(
+                out=codes[:].bitcast(FP8X4), scales=sc[:], in_=grouped[:].rearrange("p a w i -> p (a w i)")
+            )
+            w_codes[ch, g], w_sc[ch, g] = codes, sc
+
+        h_tiles = {}
+
+        def load_h(c):
+            h_tiles[c] = ring.tile([P, T], F32, name="h_tile", bufs=3)
+            nc.sync.dma_start(out=h_tiles[c][:], in_=hT[c * P : (c + 1) * P, :])
+
+        wgo_sb = keep.tile([P, J], F32, name="wgo_sb")
+
+        def sums(c, h, g):
+            ch = max(i for i in range(len(CHUNKS)) if CHUNKS[i][0] <= c * P)
+            n0, width = CHUNKS[ch]
+            acc = psum.tile([P, HALF], F32, name="acc", tag=f"acc{g}")
+            cols = slice(c * P, (c + 1) * P)
+            for a in range(PASSES):
+                nc.tensor.matmul_mx(
+                    out=acc[:],
+                    lhsT=u_codes[g][:, a, cols].bitcast(FP8X4),
+                    lhsT_scale=u_sc[g][:, a, :].bitcast(U8)[:, cols],
+                    rhs=v_codes[h][:, a * 2 * HALF : (a + 1) * 2 * HALF].bitcast(FP4X4),
+                    rhs_scale=v_sc[h][:, a, :],
+                    start=(a == 0),
+                    stop=False,
+                )
+            for a in range(PASSES):
+                wc = slice(a * width + c * P - n0, a * width + (c + 1) * P - n0)
+                nc.tensor.matmul_mx(
+                    out=acc[:],
+                    lhsT=w_codes[ch, g][:, wc].bitcast(FP8X4),
+                    lhsT_scale=w_sc[ch, g][:, wc],
+                    rhs=x_codes[:, a, h * HALF : (h + 1) * HALF].bitcast(FP8X4),
+                    rhs_scale=x_sc[:, a, h * HALF : (h + 1) * HALF],
+                    start=False,
+                    stop=(a == PASSES - 1),
+                )
+            return acc
+
+        def update(c, j0, width, eng, fused):
+            z = ring.tile([P, width], F32, name="z", bufs=2)
+            keep_gate = ring.tile([P, width], F32, name="keep_gate", bufs=2)
+            cand = ring.tile([P, width], F32, name="cand", bufs=2)
+            for h in range(j0 // HALF, (j0 + width) // HALF):
+                cols = slice(h * HALF - j0, (h + 1) * HALF - j0)
+                sz = sums(c, h, 0)
+                sn = sums(c, h, 1)
+                nc.scalar.activation(keep_gate[:, cols], sz[:], ACT.Sigmoid, bias=neg_bz[:, c : c + 1], scale=-1.0)
+                nc.scalar.activation(z[:, cols], sz[:], ACT.Sigmoid, bias=bias[0][:, c : c + 1])
+                nc.scalar.activation(cand[:, cols], sn[:], ACT.Tanh, bias=bias[1][:, c : c + 1])
+            kept = ring.tile([P, width], F32, name="kept", bufs=2)
+            nc.vector.tensor_tensor(kept[:], h_tiles[c][:].indirect(listed(j0, width)), keep_gate[:], ALU.mult)
+            new = ring.tile([P, width], F32, name="new", bufs=3)
+            eng.tensor_tensor(new[:], z[:], cand[:], ALU.mult)
+            eng.tensor_tensor(new[:], new[:], kept[:], ALU.add)
+            if not fused:
+                eng.tensor_tensor(new[:], new[:], wgo_sb[:, j0 : j0 + width], ALU.mult)
+            return new
+
+        def scatter(c, j0, width, fused, new):
+            target = windows[c % 2][:].indirect(listed(j0, width))
+            if fused:
+                nc.vector.tensor_tensor(target, new[:], wgo_sb[:, j0 : j0 + width], ALU.mult)
+            else:
+                nc.vector.tensor_copy(target, new[:])
+            if j0 + width == J:
+                nc.sync.dma_start(out=out[c * P : (c + 1) * P, :], in_=windows[c % 2][:])
+
+        def fetch(ch):
+            raws = [load_w(ch, g) for g in range(2)]
+            return raws
+
+        def prep(ch, raws):
+            for g in range(2):
+                prep_w(ch, g, raws[g])
+
+        gather_table(0)
+        x00 = load_x(0, 0)
+        raws0 = fetch(0)
+        load_u(0, 256)
+        x10 = load_x(1, 0)
+        prep_x(0, 0, x00)
+        prep(0, raws0)
+        prep_x(1, 0, x10)
+        gather_table(1)
+        load_h(0)
+        nc.sync.dma_start(out=wgo_sb[:], in_=wgo)
+        x01 = load_x(0, 1)
+        x11 = load_x(1, 1)
+
+        units = [(0, 0, HALF), (0, HALF, HALF), (1, 0, HALF), (1, HALF, HALF)] + [(c, 0, J) for c in range(2, TILES)]
+
+        def extra(i):
+            if i == 0:
+                prep_x(0, 1, x01)
+                prep_x(1, 1, x11)
+                raws = fetch(1)
+                load_h(1)
+                prep(1, raws)
+            if i == 1:
+                raws = fetch(2)
+                load_u(256, 256)
+                load_h(2)
+                prep(2, raws)
+            if i == 3:
+                load_h(3)
+                raws = fetch(3)
+                load_u(512, 256)
+                prep(3, raws)
+            if i == 4:
+                load_h(4)
+            if i == 5:
+                raws = fetch(4)
+                load_u(768, 256)
+                load_h(5)
+                prep(4, raws)
+            if i == 6:
+                load_h(6)
+            if i == 7:
+                load_h(7)
+
+        pending = None
+        for i, (c, j0, width) in enumerate(units):
+            fused = i == 0
+            new = update(c, j0, width, nc.vector if fused else nc.gpsimd, fused)
+            extra(i)
+            if pending is not None:
+                scatter(*pending)
+            pending = (c, j0, width, fused, new)
+            if fused:
+                scatter(*pending)
+                pending = None
+        scatter(*pending)

@@ -1,6 +1,7 @@
 from contextlib import ExitStack
 
 import concourse.mybir as mybir
+from concourse.masks import make_identity
 
 K, M, N, T, J = 1024, 1024, 1024, 2048, 1024
 FLOPS = 2 * 2 * (K + M) * N * J
@@ -22,6 +23,7 @@ KP = P * PACK
 PASSES = 2
 HALF = 512
 TILES = N // P
+WINDOWS = 3
 CHUNKS = [(0, 128), (128, 128), (256, 256), (512, 256), (768, 256)]
 
 
@@ -32,7 +34,8 @@ def tile_list_tgn_ema_kernel(
     with ExitStack() as ctx:
         keep = ctx.enter_context(tc.tile_pool(name="keep", bufs=1))
         ring = ctx.enter_context(tc.tile_pool(name="ring", bufs=2))
-        psum = ctx.enter_context(tc.psum_pool(name="psum", bufs=4))
+        psum = ctx.enter_context(tc.psum_pool(name="psum", bufs=1))
+        banks = [psum.tile([P, HALF], F32, name=f"bank{b}") for b in range(8)]
 
         offsets = keep.tile([P, J // 16], U16, name="offsets")
         nc.sync.dma_start(offsets[:], offs)
@@ -68,11 +71,12 @@ def tile_list_tgn_ema_kernel(
         neg_bz = keep.tile([P, TILES], F32, name="neg_bz")
         nc.vector.tensor_scalar(neg_bz[:], bias[0][:], -1.0, None, ALU.mult)
 
-        windows = []
-        for b in range(2):
-            win = keep.tile([P, T], F32, name=f"window{b}")
-            nc.gpsimd.memset(win[:], 0.0)
-            windows.append(win)
+        wgo_col = keep.tile([P, J // P], F32, name="wgo_col")
+        with nc.allow_non_contiguous_dma(reason="one weight a partition"):
+            nc.scalar.dma_start(out=wgo_col[:], in_=wgo[0].rearrange("(b p) -> p b", p=P))
+        ident = keep.tile([P, P], F32, name="ident")
+        make_identity(nc, ident[:])
+        windows = [keep.tile([P, T], F32, name=f"window{b}") for b in range(WINDOWS)]
 
         tab_w = keep.tile([P, T], I32, name="tab_w")
         nc.sync.dma_start(out=tab_w[:], in_=tab_words[0].rearrange("p t b -> p (t b)").bitcast(I32))
@@ -96,10 +100,8 @@ def tile_list_tgn_ema_kernel(
         def load_rows(raw, rows):
             nc.sync.dma_start(out=raw, in_=rows.rearrange("(p i) w -> p i w", i=PACK))
 
-        def interleave(grouped, raw):
-            nc.scalar.copy(
-                out=grouped.rearrange("p (c e) i -> p c i e", e=4), in_=raw.rearrange("p i (c e) -> p c i e", e=4)
-            )
+        def interleave(grouped, raw, copy=nc.scalar.copy):
+            copy(out=grouped.rearrange("p (c e) i -> p c i e", e=4), in_=raw.rearrange("p i (c e) -> p c i e", e=4))
 
         x_codes = keep.tile([P, PASSES, J], U32, name="x_codes", align_bytes=64)
         x_sc = keep.tile([P, PASSES, J], U8, name="x_sc", align_bytes=64)
@@ -109,9 +111,11 @@ def tile_list_tgn_ema_kernel(
             load_rows(raw[:], x[a * KP : (a + 1) * KP, h * HALF : (h + 1) * HALF])
             return raw
 
-        def prep_x(a, h, raw):
+        def prep_x(a, h, raw, share=0):
             grouped = ring.tile([P, HALF, PACK], BF16, name="x_grouped", tag="grouped", bufs=4, align_bytes=64)
-            interleave(grouped[:], raw[:])
+            interleave(grouped[:, share:, :], raw[:, :, share:])
+            if share:
+                interleave(grouped[:, :share, :], raw[:, :, :share], nc.vector.tensor_copy)
             cols = slice(h * HALF, (h + 1) * HALF)
             nc.vector.quantize_mx(
                 out=x_codes[:, a, cols].bitcast(FP8X4), scales=x_sc[:, a, cols], in_=grouped[:].rearrange("p w i -> p (w i)")
@@ -154,10 +158,9 @@ def tile_list_tgn_ema_kernel(
 
         wgo_sb = keep.tile([P, J], F32, name="wgo_sb")
 
-        def sums(c, h, g):
+        def sums(c, h, g, acc):
             ch = max(i for i in range(len(CHUNKS)) if CHUNKS[i][0] <= c * P)
             n0, width = CHUNKS[ch]
-            acc = psum.tile([P, HALF], F32, name="acc", tag=f"acc{g}")
             cols = slice(c * P, (c + 1) * P)
             for a in range(PASSES):
                 nc.tensor.matmul_mx(
@@ -182,38 +185,52 @@ def tile_list_tgn_ema_kernel(
                 )
             return acc
 
-        def update(c, j0, width, eng, fused):
-            z = ring.tile([P, width], F32, name="z", bufs=2)
-            keep_gate = ring.tile([P, width], F32, name="keep_gate", bufs=2)
-            cand = ring.tile([P, width], F32, name="cand", bufs=2)
-            for h in range(j0 // HALF, (j0 + width) // HALF):
-                cols = slice(h * HALF - j0, (h + 1) * HALF - j0)
-                sz = sums(c, h, 0)
-                sn = sums(c, h, 1)
-                nc.scalar.activation(keep_gate[:, cols], sz[:], ACT.Sigmoid, bias=neg_bz[:, c : c + 1], scale=-1.0)
-                nc.scalar.activation(z[:, cols], sz[:], ACT.Sigmoid, bias=bias[0][:, c : c + 1])
-                nc.scalar.activation(cand[:, cols], sn[:], ACT.Tanh, bias=bias[1][:, c : c + 1])
-            kept = ring.tile([P, width], F32, name="kept", bufs=2)
-            nc.vector.tensor_tensor(kept[:], h_tiles[c][:].indirect(listed(j0, width)), keep_gate[:], ALU.mult)
-            new = ring.tile([P, width], F32, name="new", bufs=3)
-            eng.tensor_tensor(new[:], z[:], cand[:], ALU.mult)
-            eng.tensor_tensor(new[:], new[:], kept[:], ALU.add)
-            if not fused:
-                eng.tensor_tensor(new[:], new[:], wgo_sb[:, j0 : j0 + width], ALU.mult)
-            return new
+        def update(c, h, pair):
+            z = ring.tile([P, HALF], F32, name="z", bufs=3)
+            keep_gate = ring.tile([P, HALF], F32, name="keep_gate", bufs=3)
+            cand = ring.tile([P, HALF], F32, name="cand", bufs=3)
+            sz = sums(c, h, 0, pair[0])
+            sn = sums(c, h, 1, pair[1])
+            nc.scalar.activation(keep_gate[:], sz[:], ACT.Sigmoid, bias=neg_bz[:, c : c + 1], scale=-1.0)
+            nc.scalar.activation(z[:], sz[:], ACT.Sigmoid, bias=bias[0][:, c : c + 1])
+            nc.scalar.activation(cand[:], sn[:], ACT.Tanh, bias=bias[1][:, c : c + 1])
+            kept = ring.tile([P, HALF], F32, name="kept", bufs=4)
+            nc.vector.tensor_tensor(kept[:], h_tiles[c][:].indirect(listed(h * HALF, HALF)), keep_gate[:], ALU.mult)
+            new = ring.tile([P, HALF], F32, name="new", bufs=4)
+            nc.vector.tensor_tensor(new[:], z[:], cand[:], ALU.mult)
+            return kept, new
 
-        def scatter(c, j0, width, fused, new):
-            target = windows[c % 2][:].indirect(listed(j0, width))
-            if fused:
-                nc.vector.tensor_tensor(target, new[:], wgo_sb[:, j0 : j0 + width], ALU.mult)
+        def add_up(h, direct, kept, new, pair):
+            total = ring.tile([P, HALF], F32, name="total", bufs=3)
+            if direct:
+                nc.vector.tensor_tensor(total[:], new[:], kept[:], ALU.add)
+                return total
+            blocks = [slice(b * P, (b + 1) * P) for b in range(HALF // P)]
+            back, turned = pair
+            for blk in blocks:
+                nc.tensor.matmul(turned[:, blk], kept[:, blk], ident[:], start=True, stop=False, is_transpose=True)
+                nc.tensor.matmul(turned[:, blk], new[:, blk], ident[:], start=False, stop=True, is_transpose=True)
+            by_event = ring.tile([P, HALF], F32, name="by_event", bufs=2)
+            for b, blk in enumerate(blocks):
+                col = h * len(blocks) + b
+                nc.scalar.activation(by_event[:, blk], turned[:, blk], ACT.Copy, scale=wgo_col[:, col : col + 1])
+            for blk in blocks:
+                nc.tensor.transpose(back[:, blk], by_event[:, blk], ident[:])
+            nc.scalar.copy(total[:], back[:])
+            return total
+
+        def scatter(c, h, direct, total):
+            window = windows[c % WINDOWS]
+            target = window[:].indirect(listed(h * HALF, HALF))
+            if direct:
+                nc.vector.tensor_tensor(target, total[:], wgo_sb[:, h * HALF : (h + 1) * HALF], ALU.mult)
             else:
-                nc.vector.tensor_copy(target, new[:])
-            if j0 + width == J:
-                nc.sync.dma_start(out=out[c * P : (c + 1) * P, :], in_=windows[c % 2][:])
+                nc.vector.tensor_copy(target, total[:])
+            if h == 1:
+                nc.sync.dma_start(out=out[c * P : (c + 1) * P, :], in_=window[:])
 
         def fetch(ch):
-            raws = [load_w(ch, g) for g in range(2)]
-            return raws
+            return [load_w(ch, g) for g in range(2)]
 
         def prep(ch, raws):
             for g in range(2):
@@ -224,55 +241,58 @@ def tile_list_tgn_ema_kernel(
         raws0 = fetch(0)
         load_u(0, 256)
         x10 = load_x(1, 0)
+        raws1 = fetch(1)
+        load_h(0)
+        nc.sync.dma_start(out=wgo_sb[:, 0:HALF], in_=wgo[:, 0:HALF])
+        load_h(1)
         prep_x(0, 0, x00)
         prep(0, raws0)
-        prep_x(1, 0, x10)
+        prep_x(1, 0, x10, 256)
         gather_table(1)
-        load_h(0)
-        nc.sync.dma_start(out=wgo_sb[:], in_=wgo)
         x01 = load_x(0, 1)
         x11 = load_x(1, 1)
+        nc.sync.dma_start(out=wgo_sb[:, HALF:J], in_=wgo[:, HALF:J])
+        for win in windows:
+            nc.vector.memset(win[:], 0.0)
 
-        units = [(0, 0, HALF), (0, HALF, HALF), (1, 0, HALF), (1, HALF, HALF)] + [(c, 0, J) for c in range(2, TILES)]
+        units = [(0, 0), (1, 0), (0, 1), (1, 1)] + [(c, h) for c in range(2, TILES) for h in range(2)]
+        DIRECT = 3
+        finish_at = {0: 0, 1: 1, 2: 2, 3: 3, 4: 5, 5: 6}
 
         def extra(i):
             if i == 0:
+                prep(1, raws1)
+            if i == 1:
                 prep_x(0, 1, x01)
                 prep_x(1, 1, x11)
-                raws = fetch(1)
-                load_h(1)
-                prep(1, raws)
-            if i == 1:
+                load_h(2)
                 raws = fetch(2)
                 load_u(256, 256)
-                load_h(2)
                 prep(2, raws)
             if i == 3:
                 load_h(3)
                 raws = fetch(3)
                 load_u(512, 256)
                 prep(3, raws)
-            if i == 4:
-                load_h(4)
             if i == 5:
+                load_h(4)
+            if i == 7:
+                load_h(5)
                 raws = fetch(4)
                 load_u(768, 256)
-                load_h(5)
                 prep(4, raws)
-            if i == 6:
+            if i == 9:
                 load_h(6)
-            if i == 7:
+            if i == 11:
                 load_h(7)
 
-        pending = None
-        for i, (c, j0, width) in enumerate(units):
-            fused = i == 0
-            new = update(c, j0, width, nc.vector if fused else nc.gpsimd, fused)
-            extra(i)
-            if pending is not None:
-                scatter(*pending)
-            pending = (c, j0, width, fused, new)
-            if fused:
-                scatter(*pending)
-                pending = None
-        scatter(*pending)
+        parts = {}
+        for step in range(len(units) + 2):
+            pair = banks[2 * (step % 4) : 2 * (step % 4) + 2]
+            if step < len(units):
+                parts[step] = update(*units[step], pair)
+            extra(step)
+            for u, (c, h) in enumerate(units):
+                if finish_at.get(u, u + 2) == step:
+                    total = add_up(h, u < DIRECT, *parts[u], pair)
+                    scatter(c, h, u < DIRECT, total)

@@ -55,6 +55,8 @@ def tile_list_tgn_ema_kernel(
         nc.vector.memset(warm[:, 0:4], 0.0)
         nc.scalar.activation(warm[:, 4:8], warm[:, 0:4], ACT.Sigmoid)
 
+        tab_w = ring.tile([P, T], I32, name="tab_w", tag="wide", bufs=4)
+        nc.sync.dma_start(out=tab_w[:], in_=tab_words[0].rearrange("p t b -> p (t b)").bitcast(I32))
         tab_sc = keep.tile([P, PASSES, T // 4], I32, name="tab_sc", align_bytes=64)
         load_scale_rows(nc.sync, tab_sc, tab_scales)
         u_sc = []
@@ -62,24 +64,21 @@ def tile_list_tgn_ema_kernel(
             plane = keep.tile([P, PASSES, N // 4], I32, name=name, align_bytes=64)
             load_scale_rows(nc.scalar, plane, scales)
             u_sc.append(plane)
-        bias = []
-        for name, vec in (("bz_sb", bz), ("bn_sb", bn)):
-            col = keep.tile([P, TILES], F32, name=name)
-            with nc.allow_non_contiguous_dma(reason="one bias value a partition"):
-                nc.scalar.dma_start(out=col[:], in_=vec.rearrange("(c p) -> p c", p=P))
-            bias.append(col)
-        neg_bz = keep.tile([P, TILES], F32, name="neg_bz")
-        nc.vector.tensor_scalar(neg_bz[:], bias[0][:], -1.0, None, ALU.mult)
-
-        wgo_col = keep.tile([P, J // P], F32, name="wgo_col")
-        with nc.allow_non_contiguous_dma(reason="one weight a partition"):
-            nc.scalar.dma_start(out=wgo_col[:], in_=wgo[0].rearrange("(b p) -> p b", p=P))
         ident = keep.tile([P, P], F32, name="ident")
         make_identity(nc, ident[:])
+        bias_rows = keep.tile([P, P], F32, name="bias_rows")
+        nc.vector.memset(bias_rows[:], 0.0)
+        nc.scalar.dma_start(out=bias_rows[0:TILES, :], in_=bz.rearrange("(c p) -> c p", p=P))
+        nc.scalar.dma_start(out=bias_rows[32 : 32 + TILES, :], in_=bn.rearrange("(c p) -> c p", p=P))
+        nc.tensor.transpose(banks[7][:, 0:P], bias_rows[:], ident[:])
+        bias_cols = keep.tile([P, 40], F32, name="bias_cols")
+        nc.scalar.copy(bias_cols[:], banks[7][:, 0:40])
+        bias = [bias_cols[:, 0:TILES], bias_cols[:, 32 : 32 + TILES]]
+        neg_bz = keep.tile([P, TILES], F32, name="neg_bz")
+        nc.scalar.activation(neg_bz[:], banks[7][:, 0:TILES], ACT.Copy, scale=-1.0)
+
         windows = [keep.tile([P, T], F32, name=f"window{b}") for b in range(WINDOWS)]
 
-        tab_w = keep.tile([P, T], I32, name="tab_w")
-        nc.sync.dma_start(out=tab_w[:], in_=tab_words[0].rearrange("p t b -> p (t b)").bitcast(I32))
 
         v_codes, v_sc = [], []
 
@@ -153,7 +152,7 @@ def tile_list_tgn_ema_kernel(
         h_tiles = {}
 
         def load_h(c):
-            h_tiles[c] = ring.tile([P, T], F32, name="h_tile", bufs=3)
+            h_tiles[c] = ring.tile([P, T], F32, name="h_tile", tag="wide", bufs=4)
             nc.sync.dma_start(out=h_tiles[c][:], in_=hT[c * P : (c + 1) * P, :])
 
         wgo_sb = keep.tile([P, J], F32, name="wgo_sb")
@@ -185,47 +184,49 @@ def tile_list_tgn_ema_kernel(
                 )
             return acc
 
-        def update(c, h, pair):
+        def multiply(c, h, pair):
+            for g in range(2):
+                sums(c, h, g, pair[g])
+
+        def gate(c, h, pair):
             z = ring.tile([P, HALF], F32, name="z", bufs=3)
             keep_gate = ring.tile([P, HALF], F32, name="keep_gate", bufs=3)
             cand = ring.tile([P, HALF], F32, name="cand", bufs=3)
-            sz = sums(c, h, 0, pair[0])
-            sn = sums(c, h, 1, pair[1])
-            nc.scalar.activation(keep_gate[:], sz[:], ACT.Sigmoid, bias=neg_bz[:, c : c + 1], scale=-1.0)
-            nc.scalar.activation(z[:], sz[:], ACT.Sigmoid, bias=bias[0][:, c : c + 1])
-            nc.scalar.activation(cand[:], sn[:], ACT.Tanh, bias=bias[1][:, c : c + 1])
+            nc.scalar.activation(keep_gate[:], pair[0][:], ACT.Sigmoid, bias=neg_bz[:, c : c + 1], scale=-1.0)
+            nc.scalar.activation(z[:], pair[0][:], ACT.Sigmoid, bias=bias[0][:, c : c + 1])
+            nc.scalar.activation(cand[:], pair[1][:], ACT.Tanh, bias=bias[1][:, c : c + 1])
             kept = ring.tile([P, HALF], F32, name="kept", bufs=4)
             nc.vector.tensor_tensor(kept[:], h_tiles[c][:].indirect(listed(h * HALF, HALF)), keep_gate[:], ALU.mult)
             new = ring.tile([P, HALF], F32, name="new", bufs=4)
             nc.vector.tensor_tensor(new[:], z[:], cand[:], ALU.mult)
             return kept, new
 
-        def add_up(h, direct, kept, new, pair):
+        blocks = [slice(b * P, (b + 1) * P) for b in range(HALF // P)]
+
+        def add_direct(kept, new):
             total = ring.tile([P, HALF], F32, name="total", bufs=3)
-            if direct:
-                nc.vector.tensor_tensor(total[:], new[:], kept[:], ALU.add)
-                return total
-            blocks = [slice(b * P, (b + 1) * P) for b in range(HALF // P)]
-            back, turned = pair
-            for blk in blocks:
-                nc.tensor.matmul(turned[:, blk], kept[:, blk], ident[:], start=True, stop=False, is_transpose=True)
-                nc.tensor.matmul(turned[:, blk], new[:, blk], ident[:], start=False, stop=True, is_transpose=True)
-            by_event = ring.tile([P, HALF], F32, name="by_event", bufs=2)
-            for b, blk in enumerate(blocks):
-                col = h * len(blocks) + b
-                nc.scalar.activation(by_event[:, blk], turned[:, blk], ACT.Copy, scale=wgo_col[:, col : col + 1])
-            for blk in blocks:
-                nc.tensor.transpose(back[:, blk], by_event[:, blk], ident[:])
-            nc.scalar.copy(total[:], back[:])
+            nc.vector.tensor_tensor(total[:], new[:], kept[:], ALU.add)
             return total
 
-        def scatter(c, h, direct, total):
+        def add_turned(kept, new, bank):
+            for blk in blocks:
+                nc.tensor.matmul(bank[:, blk], kept[:, blk], ident[:], start=True, stop=False, is_transpose=True)
+                nc.tensor.matmul(bank[:, blk], new[:, blk], ident[:], start=False, stop=True, is_transpose=True)
+            by_event = ring.tile([P, HALF], F32, name="by_event", bufs=3)
+            nc.scalar.copy(by_event[:], bank[:])
+            return by_event
+
+        def turn_back(by_event, bank):
+            for blk in blocks:
+                nc.tensor.transpose(bank[:, blk], by_event[:, blk], ident[:])
+            total = ring.tile([P, HALF], F32, name="total", bufs=3)
+            nc.scalar.copy(total[:], bank[:])
+            return total
+
+        def scatter(c, h, total):
             window = windows[c % WINDOWS]
             target = window[:].indirect(listed(h * HALF, HALF))
-            if direct:
-                nc.vector.tensor_tensor(target, total[:], wgo_sb[:, h * HALF : (h + 1) * HALF], ALU.mult)
-            else:
-                nc.vector.tensor_copy(target, total[:])
+            nc.vector.tensor_tensor(target, total[:], wgo_sb[:, h * HALF : (h + 1) * HALF], ALU.mult)
             if h == 1:
                 nc.sync.dma_start(out=out[c * P : (c + 1) * P, :], in_=window[:])
 
@@ -252,12 +253,14 @@ def tile_list_tgn_ema_kernel(
         x01 = load_x(0, 1)
         x11 = load_x(1, 1)
         nc.sync.dma_start(out=wgo_sb[:, HALF:J], in_=wgo[:, HALF:J])
+        load_h(2)
+        raws = {2: fetch(2)}
+        load_u(256, 256)
         for win in windows:
             nc.vector.memset(win[:], 0.0)
 
         units = [(0, 0), (1, 0), (0, 1), (1, 1)] + [(c, h) for c in range(2, TILES) for h in range(2)]
-        DIRECT = 3
-        finish_at = {0: 0, 1: 1, 2: 2, 3: 3, 4: 5, 5: 6}
+        DIRECT = 4
 
         def extra(i):
             if i == 0:
@@ -265,34 +268,41 @@ def tile_list_tgn_ema_kernel(
             if i == 1:
                 prep_x(0, 1, x01)
                 prep_x(1, 1, x11)
-                load_h(2)
-                raws = fetch(2)
-                load_u(256, 256)
-                prep(2, raws)
-            if i == 3:
+                prep(2, raws[2])
                 load_h(3)
-                raws = fetch(3)
-                load_u(512, 256)
-                prep(3, raws)
-            if i == 5:
+                raws[3] = fetch(3)
+                load_u(512, 512)
+            if i == 2:
                 load_h(4)
-            if i == 7:
+            if i == 3:
                 load_h(5)
-                raws = fetch(4)
-                load_u(768, 256)
-                prep(4, raws)
-            if i == 9:
+                raws[4] = fetch(4)
+            if i == 4:
+                prep(3, raws[3])
+            if i == 5:
                 load_h(6)
-            if i == 11:
+            if i == 7:
                 load_h(7)
+            if i == 8:
+                prep(4, raws[4])
 
-        parts = {}
+        def pair_of(step):
+            return banks[2 * (step % 4) : 2 * (step % 4) + 2]
+
+        parts, turned = {}, {}
+        multiply(*units[0], pair_of(0))
         for step in range(len(units) + 2):
-            pair = banks[2 * (step % 4) : 2 * (step % 4) + 2]
+            pair = pair_of(step)
             if step < len(units):
-                parts[step] = update(*units[step], pair)
+                parts[step] = gate(*units[step], pair)
             extra(step)
-            for u, (c, h) in enumerate(units):
-                if finish_at.get(u, u + 2) == step:
-                    total = add_up(h, u < DIRECT, *parts[u], pair)
-                    scatter(c, h, u < DIRECT, total)
+            if step + 1 < len(units):
+                multiply(*units[step + 1], pair_of(step + 1))
+            if step < DIRECT:
+                scatter(*units[step], add_direct(*parts[step]))
+            if step - 2 >= DIRECT:
+                total = turn_back(turned[step - 2], pair[0])
+            if DIRECT <= step - 1 < len(units):
+                turned[step - 1] = add_turned(*parts[step - 1], pair[1])
+            if step - 2 >= DIRECT:
+                scatter(*units[step - 2], total)

@@ -43,58 +43,53 @@ def tile_list_tgn_ema_kernel(
         def listed(j0, width):
             return offsets[:, j0 // 16 : (j0 + width) // 16]
 
-        def load_scale_rows(queue, plane, scales):
-            nc.vector.memset(plane[:], 0)
-            rows = scales.bitcast(I32)
-            for q in range(4):
-                queue.dma_start(
-                    out=plane[32 * q : 32 * q + 4, :, :], in_=rows[:, 4 * q : 4 * q + 4, :].rearrange("a r n -> r a n")
-                )
+        def load_scale_rows(plane, scales, q):
+            rows = scales.bitcast(I32)[:, 4 * q : 4 * q + 4, :]
+            nc.sync.dma_start(out=plane[32 * q : 32 * q + 4, :, :], in_=rows.rearrange("a r n -> r a n"))
 
+        tab_sc = keep.tile([P, PASSES, T // 4], I32, name="tab_sc", align_bytes=64)
+        u_sc = [keep.tile([P, PASSES, N // 4], I32, name=f"u_sc{g}", align_bytes=64) for g in range(2)]
+        nc.vector.memset(tab_sc[:], 0)
         warm = keep.tile([P, 8], F32, name="warm")
         nc.vector.memset(warm[:, 0:4], 0.0)
         nc.scalar.activation(warm[:, 4:8], warm[:, 0:4], ACT.Sigmoid)
-
-        tab_w = ring.tile([P, T], I32, name="tab_w", tag="wide", bufs=4)
-        nc.sync.dma_start(out=tab_w[:], in_=tab_words[0].rearrange("p t b -> p (t b)").bitcast(I32))
-        tab_sc = keep.tile([P, PASSES, T // 4], I32, name="tab_sc", align_bytes=64)
-        load_scale_rows(nc.sync, tab_sc, tab_scales)
-        u_sc = []
-        for name, scales in (("uz_sc", uz_scales), ("un_sc", un_scales)):
-            plane = keep.tile([P, PASSES, N // 4], I32, name=name, align_bytes=64)
-            load_scale_rows(nc.scalar, plane, scales)
-            u_sc.append(plane)
-        ident = keep.tile([P, P], F32, name="ident")
-        make_identity(nc, ident[:])
+        for plane in u_sc:
+            nc.vector.memset(plane[:], 0)
         bias_rows = keep.tile([P, P], F32, name="bias_rows")
         nc.vector.memset(bias_rows[:], 0.0)
-        nc.scalar.dma_start(out=bias_rows[0:TILES, :], in_=bz.rearrange("(c p) -> c p", p=P))
-        nc.scalar.dma_start(out=bias_rows[32 : 32 + TILES, :], in_=bn.rearrange("(c p) -> c p", p=P))
-        nc.tensor.transpose(banks[7][:, 0:P], bias_rows[:], ident[:])
+        ident = keep.tile([P, P], F32, name="ident")
+        make_identity(nc, ident[:])
+        tab_w = ring.tile([P, T], I32, name="tab_w", tag="wide", bufs=4)
         bias_cols = keep.tile([P, 40], F32, name="bias_cols")
-        nc.scalar.copy(bias_cols[:], banks[7][:, 0:40])
         bias = [bias_cols[:, 0:TILES], bias_cols[:, 32 : 32 + TILES]]
         neg_bz = keep.tile([P, TILES], F32, name="neg_bz")
-        nc.scalar.activation(neg_bz[:], banks[7][:, 0:TILES], ACT.Copy, scale=-1.0)
+
+        def load_bias(g):
+            nc.sync.dma_start(out=bias_rows[32 * g : 32 * g + TILES, :], in_=(bz, bn)[g].rearrange("(c p) -> c p", p=P))
+
+        def turn_bias():
+            nc.tensor.transpose(banks[7][:, 0:P], bias_rows[:], ident[:])
+            nc.scalar.copy(bias_cols[:], banks[7][:, 0:40])
+            nc.scalar.activation(neg_bz[:], banks[7][:, 0:TILES], ACT.Copy, scale=-1.0)
 
         windows = [keep.tile([P, T], F32, name=f"window{b}") for b in range(WINDOWS)]
 
 
-        v_codes, v_sc = [], []
+        v_codes, v_sc = {}, {}
 
-        def gather_table(h):
-            sc = keep.tile([P, PASSES, HALF], U8, name=f"v_sc{h}", align_bytes=64)
-            for a in range(PASSES):
-                nc.vector.tensor_copy(sc[:, a, :], tab_sc[:, a, :].bitcast(U8).indirect(listed(h * HALF, HALF)))
+        def gather_words(h):
             pairs = keep.tile([P, HALF], U32, name=f"v_pairs{h}", align_bytes=64)
             nc.vector.tensor_copy(pairs[:], tab_w[:].bitcast(U32).indirect(listed(h * HALF, HALF)))
-            codes = keep.tile([P, PASSES * 2 * HALF], U8, name=f"v_codes{h}", align_bytes=64)
+            v_codes[h] = keep.tile([P, PASSES * 2 * HALF], U8, name=f"v_codes{h}", align_bytes=64)
             nc.vector.tensor_copy(
-                codes[:].bitcast(U16).rearrange("p (a j) -> p a j", a=PASSES),
+                v_codes[h][:].bitcast(U16).rearrange("p (a j) -> p a j", a=PASSES),
                 pairs[:].bitcast(U16).rearrange("p (j a) -> p a j", a=PASSES),
             )
-            v_codes.append(codes)
-            v_sc.append(sc)
+
+        def gather_scales(h):
+            v_sc[h] = keep.tile([P, PASSES, HALF], U8, name=f"v_sc{h}", align_bytes=64)
+            for a in range(PASSES):
+                nc.vector.tensor_copy(v_sc[h][:, a, :], tab_sc[:, a, :].bitcast(U8).indirect(listed(h * HALF, HALF)))
 
         def load_rows(raw, rows):
             nc.sync.dma_start(out=raw, in_=rows.rearrange("(p i) w -> p i w", i=PACK))
@@ -106,12 +101,17 @@ def tile_list_tgn_ema_kernel(
         x_sc = keep.tile([P, PASSES, J], U8, name="x_sc", align_bytes=64)
 
         def load_x(a, h):
-            raw = ring.tile([P, PACK, HALF], F32, name="x_raw", tag="raw", bufs=5)
+            raw = ring.tile([P, PACK, HALF], F32, name="x_raw", tag="raw", bufs=4)
             load_rows(raw[:], x[a * KP : (a + 1) * KP, h * HALF : (h + 1) * HALF])
             return raw
 
-        def prep_x(a, h, raw, share=0):
-            grouped = ring.tile([P, HALF, PACK], BF16, name="x_grouped", tag="grouped", bufs=4, align_bytes=64)
+        def staging(shape, dtype, name, lend):
+            if lend is None:
+                return ring.tile(shape, dtype, name=name, tag="grouped", bufs=3, align_bytes=64)
+            return ring.tile(shape, dtype, name=name, tag=f"lent{lend}", bufs=1, align_bytes=64)
+
+        def prep_x(a, h, raw, share=0, lend=None):
+            grouped = staging([P, HALF, PACK], BF16, "x_grouped", lend)
             interleave(grouped[:, share:, :], raw[:, :, share:])
             if share:
                 interleave(grouped[:, :share, :], raw[:, :, :share], nc.vector.tensor_copy)
@@ -127,7 +127,7 @@ def tile_list_tgn_ema_kernel(
 
         def load_w(ch, g):
             n0, width = CHUNKS[ch]
-            raw = ring.tile([P, PASSES, PACK, width], F32, name="w_raw", tag="raw", bufs=5)
+            raw = ring.tile([P, PASSES, PACK, width], F32, name="w_raw", tag="raw", bufs=4)
             for a in range(PASSES):
                 load_rows(raw[:, a, :, :], w_dram[g][a * KP : (a + 1) * KP, n0 : n0 + width])
             return raw
@@ -137,9 +137,9 @@ def tile_list_tgn_ema_kernel(
                 words = u_dram[g].rearrange("a p n i -> p a (n i)")[:, :, 4 * n0 : 4 * (n0 + width)].bitcast(I32)
                 nc.sync.dma_start(out=u_codes[g][:, :, n0 : n0 + width], in_=words)
 
-        def prep_w(ch, g, raw):
+        def prep_w(ch, g, raw, lend=None):
             width = CHUNKS[ch][1]
-            grouped = ring.tile([P, PASSES, width, PACK], BF16, name="w_grouped", tag="grouped", bufs=4, align_bytes=64)
+            grouped = staging([P, PASSES, width, PACK], BF16, "w_grouped", lend)
             for a in range(PASSES):
                 interleave(grouped[:, a, :, :], raw[:, a, :, :])
             codes = keep.tile([P, PASSES * width], U32, name=f"w_codes{ch}_{g}", align_bytes=64)
@@ -203,8 +203,11 @@ def tile_list_tgn_ema_kernel(
 
         blocks = [slice(b * P, (b + 1) * P) for b in range(HALF // P)]
 
-        def add_direct(kept, new):
-            total = ring.tile([P, HALF], F32, name="total", bufs=3)
+        def add_direct(step, kept, new):
+            if step in LENT:
+                total = staging([P, HALF], F32, "total", step)
+            else:
+                total = ring.tile([P, HALF], F32, name="total", bufs=3)
             nc.vector.tensor_tensor(total[:], new[:], kept[:], ALU.add)
             return total
 
@@ -231,48 +234,74 @@ def tile_list_tgn_ema_kernel(
                 nc.sync.dma_start(out=out[c * P : (c + 1) * P, :], in_=window[:])
 
         def fetch(ch):
-            return [load_w(ch, g) for g in range(2)]
-
-        def prep(ch, raws):
+            n0, width = CHUNKS[ch]
+            if width > P:
+                return [load_w(ch, g) for g in range(2)]
+            both = ring.tile([P, 2, PASSES, PACK, width], F32, name="w_raw2", tag="raw", bufs=4)
             for g in range(2):
-                prep_w(ch, g, raws[g])
+                for a in range(PASSES):
+                    load_rows(both[:, g, a, :, :], w_dram[g][a * KP : (a + 1) * KP, n0 : n0 + width])
+            return [both[:, g] for g in range(2)]
 
-        gather_table(0)
-        x00 = load_x(0, 0)
+        def prep(ch, raws, lend=None):
+            prep_w(ch, 0, raws[0])
+            prep_w(ch, 1, raws[1], lend)
+
+        nc.sync.dma_start(out=tab_w[:], in_=tab_words[0].rearrange("p t b -> p (t b)").bitcast(I32))
         raws0 = fetch(0)
         load_u(0, 256)
+        x00 = load_x(0, 0)
+        load_scale_rows(tab_sc, tab_scales, 0)
+        load_scale_rows(tab_sc, tab_scales, 1)
+        load_scale_rows(tab_sc, tab_scales, 2)
+        load_scale_rows(tab_sc, tab_scales, 3)
+        load_bias(0)
+        load_bias(1)
         x10 = load_x(1, 0)
-        raws1 = fetch(1)
+        load_scale_rows(u_sc[0], uz_scales, 0)
+        load_scale_rows(u_sc[0], uz_scales, 1)
+        load_scale_rows(u_sc[0], uz_scales, 2)
+        load_scale_rows(u_sc[0], uz_scales, 3)
+        load_scale_rows(u_sc[1], un_scales, 0)
+        load_scale_rows(u_sc[1], un_scales, 1)
+        load_scale_rows(u_sc[1], un_scales, 2)
         load_h(0)
+        load_scale_rows(u_sc[1], un_scales, 3)
+        raws1 = fetch(1)
         nc.sync.dma_start(out=wgo_sb[:, 0:HALF], in_=wgo[:, 0:HALF])
         load_h(1)
-        prep_x(0, 0, x00)
-        prep(0, raws0)
-        prep_x(1, 0, x10, 256)
-        gather_table(1)
         x01 = load_x(0, 1)
         x11 = load_x(1, 1)
         nc.sync.dma_start(out=wgo_sb[:, HALF:J], in_=wgo[:, HALF:J])
-        load_h(2)
         raws = {2: fetch(2)}
         load_u(256, 256)
+        load_h(2)
+        gather_words(0)
+        gather_scales(0)
+        prep(0, raws0)
+        prep_x(0, 0, x00)
+        prep_x(1, 0, x10, 0)
+        turn_bias()
+        gather_words(1)
+        gather_scales(1)
         for win in windows:
             nc.vector.memset(win[:], 0.0)
 
         units = [(0, 0), (1, 0), (0, 1), (1, 1)] + [(c, h) for c in range(2, TILES) for h in range(2)]
-        DIRECT = 4
+        DIRECT = 3
+        LENT = (0, 1, 2)
 
         def extra(i):
             if i == 0:
-                prep(1, raws1)
+                prep(1, raws1, 0)
             if i == 1:
                 prep_x(0, 1, x01)
-                prep_x(1, 1, x11)
-                prep(2, raws[2])
+                prep_x(1, 1, x11, 0, 1)
                 load_h(3)
                 raws[3] = fetch(3)
                 load_u(512, 512)
             if i == 2:
+                prep(2, raws[2], 2)
                 load_h(4)
             if i == 3:
                 load_h(5)
@@ -299,7 +328,7 @@ def tile_list_tgn_ema_kernel(
             if step + 1 < len(units):
                 multiply(*units[step + 1], pair_of(step + 1))
             if step < DIRECT:
-                scatter(*units[step], add_direct(*parts[step]))
+                scatter(*units[step], add_direct(step, *parts[step]))
             if step - 2 >= DIRECT:
                 total = turn_back(turned[step - 2], pair[0])
             if DIRECT <= step - 1 < len(units):

@@ -24,7 +24,9 @@ PASSES = 2
 HALF = 512
 TILES = N // P
 WINDOWS = 3
-CHUNKS = [(0, 128), (128, 128), (256, 256), (512, 256), (768, 256)]
+CHUNK = 256
+QUARTER = 256
+RAW = 5
 
 
 def tile_list_tgn_ema_kernel(
@@ -43,39 +45,60 @@ def tile_list_tgn_ema_kernel(
         def listed(j0, width):
             return offsets[:, j0 // 16 : (j0 + width) // 16]
 
-        def load_scale_rows(plane, scales, q):
-            rows = scales.bitcast(I32)[:, 4 * q : 4 * q + 4, :]
-            nc.sync.dma_start(out=plane[32 * q : 32 * q + 4, :, :], in_=rows.rearrange("a r n -> r a n"))
+        def load_scale_rows(plane, scales, q, n0, width):
+            rows = scales.bitcast(I32)[:, 4 * q : 4 * q + 4, n0 // 4 : (n0 + width) // 4]
+            nc.gpsimd.dma_start(
+                out=plane[32 * q : 32 * q + 4, :, n0 // 4 : (n0 + width) // 4], in_=rows.rearrange("a r n -> r a n")
+            )
 
-        tab_sc = keep.tile([P, PASSES, T // 4], I32, name="tab_sc", align_bytes=64)
+        def load_table_scales(q):
+            nc.sync.dma_start(out=tab_sc[32 * q : 32 * q + 8, :], in_=tab_scales.bitcast(I32)[:, 4 * q : 4 * q + 4, :])
+
+        tab_sc = keep.tile([P, T // 4], I32, name="tab_sc", align_bytes=64)
         u_sc = [keep.tile([P, PASSES, N // 4], I32, name=f"u_sc{g}", align_bytes=64) for g in range(2)]
         nc.vector.memset(tab_sc[:], 0)
+        v_sc = [keep.tile([P, J], U8, name=f"v_sc{a}", align_bytes=64) for a in range(PASSES)]
+        nc.vector.memset(v_sc[1][:].bitcast(I32), 0)
         warm = keep.tile([P, 8], F32, name="warm")
         nc.vector.memset(warm[:, 0:4], 0.0)
         nc.scalar.activation(warm[:, 4:8], warm[:, 0:4], ACT.Sigmoid)
-        for plane in u_sc:
+        for plane, scales in zip(u_sc, (uz_scales, un_scales)):
             nc.vector.memset(plane[:], 0)
+            for q in range(4):
+                load_scale_rows(plane, scales, q, 0, N)
         bias_rows = keep.tile([P, P], F32, name="bias_rows")
         nc.vector.memset(bias_rows[:], 0.0)
         ident = keep.tile([P, P], F32, name="ident")
         make_identity(nc, ident[:])
         tab_w = ring.tile([P, T], I32, name="tab_w", tag="wide", bufs=4)
-        bias_cols = keep.tile([P, 40], F32, name="bias_cols")
+        bias_cols = keep.tile([P, 72], F32, name="bias_cols")
         bias = [bias_cols[:, 0:TILES], bias_cols[:, 32 : 32 + TILES]]
         neg_bz = keep.tile([P, TILES], F32, name="neg_bz")
 
         def load_bias(g):
             nc.sync.dma_start(out=bias_rows[32 * g : 32 * g + TILES, :], in_=(bz, bn)[g].rearrange("(c p) -> c p", p=P))
 
+        def load_event_weights():
+            nc.sync.dma_start(out=bias_rows[64 : 64 + J // P, :], in_=wgo[0, :].rearrange("(c p) -> c p", p=P))
+
+        def spread_event_weights():
+            for h in range(2):
+                for b in range(HALF // P):
+                    col = 64 + h * (HALF // P) + b
+                    nc.tensor.transpose(
+                        banks[5 + h][:, b * P : (b + 1) * P], bias_cols[:, col : col + 1].to_broadcast([P, P]), ident[:]
+                    )
+                nc.scalar.copy(wgo_sb[:, h * HALF : (h + 1) * HALF], banks[5 + h][:])
+
         def turn_bias():
             nc.tensor.transpose(banks[7][:, 0:P], bias_rows[:], ident[:])
-            nc.scalar.copy(bias_cols[:], banks[7][:, 0:40])
+            nc.scalar.copy(bias_cols[:], banks[7][:, 0:72])
             nc.scalar.activation(neg_bz[:], banks[7][:, 0:TILES], ACT.Copy, scale=-1.0)
 
         windows = [keep.tile([P, T], F32, name=f"window{b}") for b in range(WINDOWS)]
 
 
-        v_codes, v_sc = {}, {}
+        v_codes = {}
 
         def gather_words(h):
             pairs = keep.tile([P, HALF], U32, name=f"v_pairs{h}", align_bytes=64)
@@ -86,10 +109,11 @@ def tile_list_tgn_ema_kernel(
                 pairs[:].bitcast(U16).rearrange("p (j a) -> p a j", a=PASSES),
             )
 
-        def gather_scales(h):
-            v_sc[h] = keep.tile([P, PASSES, HALF], U8, name=f"v_sc{h}", align_bytes=64)
-            for a in range(PASSES):
-                nc.vector.tensor_copy(v_sc[h][:, a, :], tab_sc[:, a, :].bitcast(U8).indirect(listed(h * HALF, HALF)))
+        def gather_scales():
+            nc.vector.tensor_copy(v_sc[0][:], tab_sc[:].bitcast(U8).indirect(offsets[:]))
+
+        def lower_scales():
+            nc.sync.dma_start(out=v_sc[1][0:112, :].bitcast(I32), in_=v_sc[0][4:116, :].bitcast(I32))
 
         def load_rows(raw, rows):
             nc.sync.dma_start(out=raw, in_=rows.rearrange("(p i) w -> p i w", i=PACK))
@@ -100,54 +124,57 @@ def tile_list_tgn_ema_kernel(
         x_codes = keep.tile([P, PASSES, J], U32, name="x_codes", align_bytes=64)
         x_sc = keep.tile([P, PASSES, J], U8, name="x_sc", align_bytes=64)
 
-        def load_x(a, h):
-            raw = ring.tile([P, PACK, HALF], F32, name="x_raw", tag="raw", bufs=4)
-            load_rows(raw[:], x[a * KP : (a + 1) * KP, h * HALF : (h + 1) * HALF])
+        def load_x_quarter(j0):
+            raw = ring.tile([P, PASSES, PACK, QUARTER], F32, name="x_raw", tag="raw", bufs=RAW)
+            for a in range(PASSES):
+                load_rows(raw[:, a, :, :], x[a * KP : (a + 1) * KP, j0 : j0 + QUARTER])
+            return [raw[:, a, :, :] for a in range(PASSES)]
+
+        def load_x_half(a, j0):
+            raw = ring.tile([P, PACK, HALF], F32, name="x_raw", tag="raw", bufs=RAW)
+            load_rows(raw[:], x[a * KP : (a + 1) * KP, j0 : j0 + HALF])
             return raw
 
         def staging(shape, dtype, name, lend):
             if lend is None:
-                return ring.tile(shape, dtype, name=name, tag="grouped", bufs=3, align_bytes=64)
+                return ring.tile(shape, dtype, name=name, tag="grouped", bufs=4, align_bytes=64)
             return ring.tile(shape, dtype, name=name, tag=f"lent{lend}", bufs=1, align_bytes=64)
 
-        def prep_x(a, h, raw, share=0, lend=None):
-            grouped = staging([P, HALF, PACK], BF16, "x_grouped", lend)
-            interleave(grouped[:, share:, :], raw[:, :, share:])
-            if share:
-                interleave(grouped[:, :share, :], raw[:, :, :share], nc.vector.tensor_copy)
-            cols = slice(h * HALF, (h + 1) * HALF)
-            nc.vector.quantize_mx(
-                out=x_codes[:, a, cols].bitcast(FP8X4), scales=x_sc[:, a, cols], in_=grouped[:].rearrange("p w i -> p (w i)")
-            )
+        def prep_x(a, h, raw, lend=None, copy=nc.scalar.copy):
+            for s0 in range(0, HALF, QUARTER):
+                grouped = staging([P, QUARTER, PACK], BF16, "x_grouped", lend if s0 else None)
+                interleave(grouped[:], raw[:, :, s0 : s0 + QUARTER], copy)
+                cols = slice(h * HALF + s0, h * HALF + s0 + QUARTER)
+                nc.vector.quantize_mx(
+                    out=x_codes[:, a, cols].bitcast(FP8X4), scales=x_sc[:, a, cols], in_=grouped[:].rearrange("p w i -> p (w i)")
+                )
 
         w_dram = (wz, wn)
         u_dram = (uz_words, un_words)
         u_codes = [keep.tile([P, PASSES, N], I32, name=f"u_codes{g}", align_bytes=64) for g in range(2)]
-        w_codes, w_sc = {}, {}
+        w_raw, w_codes, w_sc = {}, {}, {}
 
         def load_w(ch, g):
-            n0, width = CHUNKS[ch]
-            raw = ring.tile([P, PASSES, PACK, width], F32, name="w_raw", tag="raw", bufs=4)
+            raw = ring.tile([P, PASSES, PACK, CHUNK], F32, name="w_raw", tag="raw", bufs=RAW)
             for a in range(PASSES):
-                load_rows(raw[:, a, :, :], w_dram[g][a * KP : (a + 1) * KP, n0 : n0 + width])
-            return raw
+                load_rows(raw[:, a, :, :], w_dram[g][a * KP : (a + 1) * KP, ch * CHUNK : (ch + 1) * CHUNK])
+            w_raw[ch, g] = raw
 
-        def load_u(n0, width):
-            for g in range(2):
-                words = u_dram[g].rearrange("a p n i -> p a (n i)")[:, :, 4 * n0 : 4 * (n0 + width)].bitcast(I32)
-                nc.sync.dma_start(out=u_codes[g][:, :, n0 : n0 + width], in_=words)
+        def load_u(g, n0, width):
+            words = u_dram[g].rearrange("a p n i -> p a (n i)")[:, :, 4 * n0 : 4 * (n0 + width)].bitcast(I32)
+            nc.sync.dma_start(out=u_codes[g][:, :, n0 : n0 + width], in_=words)
 
-        def prep_w(ch, g, raw, lend=None):
-            width = CHUNKS[ch][1]
-            grouped = staging([P, PASSES, width, PACK], BF16, "w_grouped", lend)
+        def prep_w(c, g, lend=None):
+            raw, n0 = w_raw[c * P // CHUNK, g], c * P % CHUNK
+            grouped = staging([P, PASSES, P, PACK], BF16, "w_grouped", lend)
             for a in range(PASSES):
-                interleave(grouped[:, a, :, :], raw[:, a, :, :])
-            codes = keep.tile([P, PASSES * width], U32, name=f"w_codes{ch}_{g}", align_bytes=64)
-            sc = keep.tile([P, PASSES * width], U8, name=f"w_sc{ch}_{g}", align_bytes=64)
+                interleave(grouped[:, a, :, :], raw[:, a, :, n0 : n0 + P])
+            codes = keep.tile([P, PASSES * P], U32, name=f"w_codes{c}_{g}", align_bytes=64)
+            sc = keep.tile([P, PASSES * P], U8, name=f"w_sc{c}_{g}", align_bytes=64)
             nc.vector.quantize_mx(
                 out=codes[:].bitcast(FP8X4), scales=sc[:], in_=grouped[:].rearrange("p a w i -> p (a w i)")
             )
-            w_codes[ch, g], w_sc[ch, g] = codes, sc
+            w_codes[c, g], w_sc[c, g] = codes, sc
 
         h_tiles = {}
 
@@ -157,57 +184,58 @@ def tile_list_tgn_ema_kernel(
 
         wgo_sb = keep.tile([P, J], F32, name="wgo_sb")
 
-        def sums(c, h, g, acc):
-            ch = max(i for i in range(len(CHUNKS)) if CHUNKS[i][0] <= c * P)
-            n0, width = CHUNKS[ch]
+        def sums(c, j0, width, g, acc):
             cols = slice(c * P, (c + 1) * P)
+            h, t0 = divmod(j0, HALF)
+            run = width if width == HALF else P
             for a in range(PASSES):
-                nc.tensor.matmul_mx(
-                    out=acc[:],
-                    lhsT=u_codes[g][:, a, cols].bitcast(FP8X4),
-                    lhsT_scale=u_sc[g][:, a, :].bitcast(U8)[:, cols],
-                    rhs=v_codes[h][:, a * 2 * HALF : (a + 1) * 2 * HALF].bitcast(FP4X4),
-                    rhs_scale=v_sc[h][:, a, :],
-                    start=(a == 0),
-                    stop=False,
-                )
+                for r0 in range(0, width, run):
+                    v0 = t0 + r0
+                    nc.tensor.matmul_mx(
+                        out=acc[:, r0 : r0 + run],
+                        lhsT=u_codes[g][:, a, cols].bitcast(FP8X4),
+                        lhsT_scale=u_sc[g][:, a, :].bitcast(U8)[:, cols],
+                        rhs=v_codes[h][:, 2 * (a * HALF + v0) : 2 * (a * HALF + v0 + run)].bitcast(FP4X4),
+                        rhs_scale=v_sc[a][:, j0 + r0 : j0 + r0 + run],
+                        start=(a == 0 and r0 == 0),
+                        stop=False,
+                    )
             for a in range(PASSES):
-                wc = slice(a * width + c * P - n0, a * width + (c + 1) * P - n0)
+                wc = slice(a * P, (a + 1) * P)
                 nc.tensor.matmul_mx(
-                    out=acc[:],
-                    lhsT=w_codes[ch, g][:, wc].bitcast(FP8X4),
-                    lhsT_scale=w_sc[ch, g][:, wc],
-                    rhs=x_codes[:, a, h * HALF : (h + 1) * HALF].bitcast(FP8X4),
-                    rhs_scale=x_sc[:, a, h * HALF : (h + 1) * HALF],
+                    out=acc[:, 0:width],
+                    lhsT=w_codes[c, g][:, wc].bitcast(FP8X4),
+                    lhsT_scale=w_sc[c, g][:, wc],
+                    rhs=x_codes[:, a, j0 : j0 + width].bitcast(FP8X4),
+                    rhs_scale=x_sc[:, a, j0 : j0 + width],
                     start=False,
                     stop=(a == PASSES - 1),
                 )
-            return acc
 
-        def multiply(c, h, pair):
+        def multiply(unit, pair):
             for g in range(2):
-                sums(c, h, g, pair[g])
+                sums(*unit, g, pair[g])
 
-        def gate(c, h, pair):
-            z = ring.tile([P, HALF], F32, name="z", bufs=3)
-            keep_gate = ring.tile([P, HALF], F32, name="keep_gate", bufs=3)
-            cand = ring.tile([P, HALF], F32, name="cand", bufs=3)
-            nc.scalar.activation(keep_gate[:], pair[0][:], ACT.Sigmoid, bias=neg_bz[:, c : c + 1], scale=-1.0)
-            nc.scalar.activation(z[:], pair[0][:], ACT.Sigmoid, bias=bias[0][:, c : c + 1])
-            nc.scalar.activation(cand[:], pair[1][:], ACT.Tanh, bias=bias[1][:, c : c + 1])
-            kept = ring.tile([P, HALF], F32, name="kept", bufs=4)
-            nc.vector.tensor_tensor(kept[:], h_tiles[c][:].indirect(listed(h * HALF, HALF)), keep_gate[:], ALU.mult)
-            new = ring.tile([P, HALF], F32, name="new", bufs=4)
+        def gate(c, j0, width, pair):
+            z = ring.tile([P, width], F32, name="z", bufs=3)
+            keep_gate = ring.tile([P, width], F32, name="keep_gate", bufs=3)
+            cand = ring.tile([P, width], F32, name="cand", bufs=3)
+            nc.scalar.activation(keep_gate[:], pair[0][:, 0:width], ACT.Sigmoid, bias=neg_bz[:, c : c + 1], scale=-1.0)
+            nc.scalar.activation(z[:], pair[0][:, 0:width], ACT.Sigmoid, bias=bias[0][:, c : c + 1])
+            nc.scalar.activation(cand[:], pair[1][:, 0:width], ACT.Tanh, bias=bias[1][:, c : c + 1])
+            kept = ring.tile([P, width], F32, name="kept", bufs=4)
+            nc.vector.tensor_tensor(kept[:], h_tiles[c][:].indirect(listed(j0, width)), keep_gate[:], ALU.mult)
+            new = ring.tile([P, width], F32, name="new", bufs=4)
             nc.vector.tensor_tensor(new[:], z[:], cand[:], ALU.mult)
             return kept, new
 
         blocks = [slice(b * P, (b + 1) * P) for b in range(HALF // P)]
 
-        def add_direct(step, kept, new):
+        def add_direct(step, width, kept, new):
             if step in LENT:
-                total = staging([P, HALF], F32, "total", step)
+                total = staging([P, width], F32, "total", step)
             else:
-                total = ring.tile([P, HALF], F32, name="total", bufs=3)
+                total = ring.tile([P, width], F32, name="total", bufs=3)
             nc.vector.tensor_tensor(total[:], new[:], kept[:], ALU.add)
             return total
 
@@ -226,109 +254,90 @@ def tile_list_tgn_ema_kernel(
             nc.scalar.copy(total[:], bank[:])
             return total
 
-        def scatter(c, h, total):
+        def scatter(c, j0, width, total):
             window = windows[c % WINDOWS]
-            target = window[:].indirect(listed(h * HALF, HALF))
-            nc.vector.tensor_tensor(target, total[:], wgo_sb[:, h * HALF : (h + 1) * HALF], ALU.mult)
-            if h == 1:
+            target = window[:].indirect(listed(j0, width))
+            nc.vector.tensor_tensor(target, total[:], wgo_sb[:, j0 : j0 + width], ALU.mult)
+            if j0 + width == J:
                 nc.sync.dma_start(out=out[c * P : (c + 1) * P, :], in_=window[:])
 
-        def fetch(ch):
-            n0, width = CHUNKS[ch]
-            if width > P:
-                return [load_w(ch, g) for g in range(2)]
-            both = ring.tile([P, 2, PASSES, PACK, width], F32, name="w_raw2", tag="raw", bufs=4)
-            for g in range(2):
-                for a in range(PASSES):
-                    load_rows(both[:, g, a, :, :], w_dram[g][a * KP : (a + 1) * KP, n0 : n0 + width])
-            return [both[:, g] for g in range(2)]
-
-        def prep(ch, raws, lend=None):
-            prep_w(ch, 0, raws[0])
-            prep_w(ch, 1, raws[1], lend)
-
         nc.sync.dma_start(out=tab_w[:], in_=tab_words[0].rearrange("p t b -> p (t b)").bitcast(I32))
-        raws0 = fetch(0)
-        load_u(0, 256)
-        x00 = load_x(0, 0)
-        load_scale_rows(tab_sc, tab_scales, 0)
-        load_scale_rows(tab_sc, tab_scales, 1)
-        load_scale_rows(tab_sc, tab_scales, 2)
-        load_scale_rows(tab_sc, tab_scales, 3)
+        for q in range(4):
+            load_table_scales(q)
+        x_early = [load_x_half(a, 0) for a in range(PASSES)]
         load_bias(0)
         load_bias(1)
-        x10 = load_x(1, 0)
-        load_scale_rows(u_sc[0], uz_scales, 0)
-        load_scale_rows(u_sc[0], uz_scales, 1)
-        load_scale_rows(u_sc[0], uz_scales, 2)
-        load_scale_rows(u_sc[0], uz_scales, 3)
-        load_scale_rows(u_sc[1], un_scales, 0)
-        load_scale_rows(u_sc[1], un_scales, 1)
-        load_scale_rows(u_sc[1], un_scales, 2)
-        load_h(0)
-        load_scale_rows(u_sc[1], un_scales, 3)
-        raws1 = fetch(1)
-        nc.sync.dma_start(out=wgo_sb[:, 0:HALF], in_=wgo[:, 0:HALF])
-        load_h(1)
-        x01 = load_x(0, 1)
-        x11 = load_x(1, 1)
-        nc.sync.dma_start(out=wgo_sb[:, HALF:J], in_=wgo[:, HALF:J])
-        raws = {2: fetch(2)}
-        load_u(256, 256)
-        load_h(2)
+        load_event_weights()
+        load_w(0, 0)
+        load_u(0, 0, CHUNK)
         gather_words(0)
-        gather_scales(0)
-        prep(0, raws0)
-        prep_x(0, 0, x00)
-        prep_x(1, 0, x10, 0)
+        gather_scales()
+        lower_scales()
+        load_h(0)
+        load_u(1, 0, CHUNK)
+        load_w(0, 1)
+        load_h(1)
+        x_late = [load_x_half(a, HALF) for a in range(PASSES)]
+        load_w(1, 0)
+        load_w(1, 1)
+        load_u(0, CHUNK, CHUNK)
+        load_u(1, CHUNK, CHUNK)
+        load_h(2)
+        for a in range(PASSES):
+            prep_x(a, 0, x_early[a])
         turn_bias()
+        spread_event_weights()
+        prep_w(0, 0)
+        prep_w(0, 1)
+        prep_w(1, 0)
+        prep_w(1, 1)
         gather_words(1)
-        gather_scales(1)
         for win in windows:
             nc.vector.memset(win[:], 0.0)
 
-        units = [(0, 0), (1, 0), (0, 1), (1, 1)] + [(c, h) for c in range(2, TILES) for h in range(2)]
+        units = [(0, 0, HALF), (1, 0, HALF), (0, HALF, HALF), (1, HALF, HALF)]
+        units = units + [(c, h * HALF, HALF) for c in range(2, TILES) for h in range(2)]
         DIRECT = 3
-        LENT = (0, 1, 2)
+        LENT = (1, 2)
 
         def extra(i):
-            if i == 0:
-                prep(1, raws1, 0)
             if i == 1:
-                prep_x(0, 1, x01)
-                prep_x(1, 1, x11, 0, 1)
-                load_h(3)
-                raws[3] = fetch(3)
-                load_u(512, 512)
+                prep_x(0, 1, x_late[0])
+                prep_x(1, 1, x_late[1], 1, nc.vector.tensor_copy)
             if i == 2:
-                prep(2, raws[2], 2)
-                load_h(4)
+                prep_w(2, 0)
+                prep_w(2, 1, 2)
+                load_h(3)
+                load_w(2, 0)
+                load_w(2, 1)
+                load_u(0, HALF, HALF)
+                load_u(1, HALF, HALF)
             if i == 3:
+                load_h(4)
                 load_h(5)
-                raws[4] = fetch(4)
-            if i == 4:
-                prep(3, raws[3])
+                load_w(3, 0)
+                load_w(3, 1)
+            if 3 <= i < 13:
+                prep_w((i + 3) // 2, (i + 1) % 2)
             if i == 5:
                 load_h(6)
             if i == 7:
                 load_h(7)
-            if i == 8:
-                prep(4, raws[4])
 
         def pair_of(step):
             return banks[2 * (step % 4) : 2 * (step % 4) + 2]
 
         parts, turned = {}, {}
-        multiply(*units[0], pair_of(0))
+        multiply(units[0], pair_of(0))
         for step in range(len(units) + 2):
             pair = pair_of(step)
             if step < len(units):
                 parts[step] = gate(*units[step], pair)
             extra(step)
             if step + 1 < len(units):
-                multiply(*units[step + 1], pair_of(step + 1))
+                multiply(units[step + 1], pair_of(step + 1))
             if step < DIRECT:
-                scatter(*units[step], add_direct(step, *parts[step]))
+                scatter(*units[step], add_direct(step, units[step][2], *parts[step]))
             if step - 2 >= DIRECT:
                 total = turn_back(turned[step - 2], pair[0])
             if DIRECT <= step - 1 < len(units):

@@ -22,11 +22,14 @@ PACK = 4
 KP = P * PACK
 PASSES = 2
 HALF = 512
+QUARTER = 256
+CHUNK = 256
 TILES = N // P
 WINDOWS = 3
-CHUNK = 256
-QUARTER = 256
 RAW = 5
+WIDE = 4
+DIRECT = 3
+BN_ROW, WGO_ROW = 32, 64
 
 
 def tile_list_tgn_ema_kernel(
@@ -42,67 +45,54 @@ def tile_list_tgn_ema_kernel(
         offsets = keep.tile([P, J // 16], U16, name="offsets")
         nc.sync.dma_start(offsets[:], offs)
 
-        def listed(j0, width):
-            return offsets[:, j0 // 16 : (j0 + width) // 16]
-
-        def load_scale_rows(plane, scales, q, n0, width):
-            rows = scales.bitcast(I32)[:, 4 * q : 4 * q + 4, n0 // 4 : (n0 + width) // 4]
-            nc.gpsimd.dma_start(
-                out=plane[32 * q : 32 * q + 4, :, n0 // 4 : (n0 + width) // 4], in_=rows.rearrange("a r n -> r a n")
-            )
-
-        def load_table_scales(q):
-            nc.sync.dma_start(out=tab_sc[32 * q : 32 * q + 8, :], in_=tab_scales.bitcast(I32)[:, 4 * q : 4 * q + 4, :])
+        def listed(h):
+            return offsets[:, h * HALF // 16 : (h + 1) * HALF // 16]
 
         tab_sc = keep.tile([P, T // 4], I32, name="tab_sc", align_bytes=64)
         u_sc = [keep.tile([P, PASSES, N // 4], I32, name=f"u_sc{g}", align_bytes=64) for g in range(2)]
         nc.vector.memset(tab_sc[:], 0)
         v_sc = [keep.tile([P, J], U8, name=f"v_sc{a}", align_bytes=64) for a in range(PASSES)]
         nc.vector.memset(v_sc[1][:].bitcast(I32), 0)
-        warm = keep.tile([P, 8], F32, name="warm")
-        nc.vector.memset(warm[:, 0:4], 0.0)
-        nc.scalar.activation(warm[:, 4:8], warm[:, 0:4], ACT.Sigmoid)
-        for plane, scales in zip(u_sc, (uz_scales, un_scales)):
-            nc.vector.memset(plane[:], 0)
-            for q in range(4):
-                load_scale_rows(plane, scales, q, 0, N)
-        bias_rows = keep.tile([P, P], F32, name="bias_rows")
-        nc.vector.memset(bias_rows[:], 0.0)
+        for sc_tile, scales in zip(u_sc, (uz_scales, un_scales)):
+            nc.vector.memset(sc_tile[:], 0)
+            for quad in range(4):
+                rows = scales.bitcast(I32)[:, 4 * quad : 4 * quad + 4, :]
+                nc.gpsimd.dma_start(out=sc_tile[32 * quad : 32 * quad + 4, :, :], in_=rows.rearrange("a r n -> r a n"))
+
+        small_rows = keep.tile([P, P], F32, name="small_rows")
+        nc.vector.memset(small_rows[:], 0.0)
         ident = keep.tile([P, P], F32, name="ident")
         make_identity(nc, ident[:])
-        tab_w = ring.tile([P, T], I32, name="tab_w", tag="wide", bufs=4)
-        bias_cols = keep.tile([P, 72], F32, name="bias_cols")
-        bias = [bias_cols[:, 0:TILES], bias_cols[:, 32 : 32 + TILES]]
+        tab_w = ring.tile([P, T], I32, name="tab_w", tag="wide", bufs=WIDE)
+        small_cols = keep.tile([P, WGO_ROW + J // P], F32, name="small_cols")
+        bias = [small_cols[:, 0:TILES], small_cols[:, BN_ROW : BN_ROW + TILES]]
         neg_bz = keep.tile([P, TILES], F32, name="neg_bz")
+        wgo_sb = keep.tile([P, J], F32, name="wgo_sb")
 
-        def load_bias(g):
-            nc.sync.dma_start(out=bias_rows[32 * g : 32 * g + TILES, :], in_=(bz, bn)[g].rearrange("(c p) -> c p", p=P))
+        def load_small(row, vector):
+            nc.sync.dma_start(out=small_rows[row : row + TILES, :], in_=vector.rearrange("(c p) -> c p", p=P))
 
-        def load_event_weights():
-            nc.sync.dma_start(out=bias_rows[64 : 64 + J // P, :], in_=wgo[0, :].rearrange("(c p) -> c p", p=P))
+        def turn_small():
+            nc.tensor.transpose(banks[7][:, 0:P], small_rows[:], ident[:])
+            nc.scalar.copy(small_cols[:], banks[7][:, 0 : WGO_ROW + J // P])
+            nc.scalar.activation(neg_bz[:], banks[7][:, 0:TILES], ACT.Copy, scale=-1.0)
 
         def spread_event_weights():
             for h in range(2):
                 for b in range(HALF // P):
-                    col = 64 + h * (HALF // P) + b
+                    col = WGO_ROW + h * (HALF // P) + b
                     nc.tensor.transpose(
-                        banks[5 + h][:, b * P : (b + 1) * P], bias_cols[:, col : col + 1].to_broadcast([P, P]), ident[:]
+                        banks[5 + h][:, b * P : (b + 1) * P], small_cols[:, col : col + 1].to_broadcast([P, P]), ident[:]
                     )
                 nc.scalar.copy(wgo_sb[:, h * HALF : (h + 1) * HALF], banks[5 + h][:])
 
-        def turn_bias():
-            nc.tensor.transpose(banks[7][:, 0:P], bias_rows[:], ident[:])
-            nc.scalar.copy(bias_cols[:], banks[7][:, 0:72])
-            nc.scalar.activation(neg_bz[:], banks[7][:, 0:TILES], ACT.Copy, scale=-1.0)
-
         windows = [keep.tile([P, T], F32, name=f"window{b}") for b in range(WINDOWS)]
-
 
         v_codes = {}
 
         def gather_words(h):
             pairs = keep.tile([P, HALF], U32, name=f"v_pairs{h}", align_bytes=64)
-            nc.vector.tensor_copy(pairs[:], tab_w[:].bitcast(U32).indirect(listed(h * HALF, HALF)))
+            nc.vector.tensor_copy(pairs[:], tab_w[:].bitcast(U32).indirect(listed(h)))
             v_codes[h] = keep.tile([P, PASSES * 2 * HALF], U8, name=f"v_codes{h}", align_bytes=64)
             nc.vector.tensor_copy(
                 v_codes[h][:].bitcast(U16).rearrange("p (a j) -> p a j", a=PASSES),
@@ -111,38 +101,30 @@ def tile_list_tgn_ema_kernel(
 
         def gather_scales():
             nc.vector.tensor_copy(v_sc[0][:], tab_sc[:].bitcast(U8).indirect(offsets[:]))
-
-        def lower_scales():
             nc.sync.dma_start(out=v_sc[1][0:112, :].bitcast(I32), in_=v_sc[0][4:116, :].bitcast(I32))
 
         def load_rows(raw, rows):
             nc.sync.dma_start(out=raw, in_=rows.rearrange("(p i) w -> p i w", i=PACK))
 
-        def interleave(grouped, raw, copy=nc.scalar.copy):
+        def interleave(grouped, raw, copy):
             copy(out=grouped.rearrange("p (c e) i -> p c i e", e=4), in_=raw.rearrange("p i (c e) -> p c i e", e=4))
+
+        def staging(shape, dtype, name, shared):
+            if shared is None:
+                return ring.tile(shape, dtype, name=name, tag="grouped", bufs=4, align_bytes=64)
+            return ring.tile(shape, dtype, name=name, tag=f"shared{shared}", bufs=1, align_bytes=64)
 
         x_codes = keep.tile([P, PASSES, J], U32, name="x_codes", align_bytes=64)
         x_sc = keep.tile([P, PASSES, J], U8, name="x_sc", align_bytes=64)
 
-        def load_x_quarter(j0):
-            raw = ring.tile([P, PASSES, PACK, QUARTER], F32, name="x_raw", tag="raw", bufs=RAW)
-            for a in range(PASSES):
-                load_rows(raw[:, a, :, :], x[a * KP : (a + 1) * KP, j0 : j0 + QUARTER])
-            return [raw[:, a, :, :] for a in range(PASSES)]
-
-        def load_x_half(a, j0):
+        def load_x(a, h):
             raw = ring.tile([P, PACK, HALF], F32, name="x_raw", tag="raw", bufs=RAW)
-            load_rows(raw[:], x[a * KP : (a + 1) * KP, j0 : j0 + HALF])
+            load_rows(raw[:], x[a * KP : (a + 1) * KP, h * HALF : (h + 1) * HALF])
             return raw
 
-        def staging(shape, dtype, name, lend):
-            if lend is None:
-                return ring.tile(shape, dtype, name=name, tag="grouped", bufs=4, align_bytes=64)
-            return ring.tile(shape, dtype, name=name, tag=f"lent{lend}", bufs=1, align_bytes=64)
-
-        def prep_x(a, h, raw, lend=None, copy=nc.scalar.copy):
+        def prep_x(a, h, raw, shared=None, copy=nc.scalar.copy):
             for s0 in range(0, HALF, QUARTER):
-                grouped = staging([P, QUARTER, PACK], BF16, "x_grouped", lend if s0 else None)
+                grouped = staging([P, QUARTER, PACK], BF16, "x_grouped", shared if s0 + QUARTER == HALF else None)
                 interleave(grouped[:], raw[:, :, s0 : s0 + QUARTER], copy)
                 cols = slice(h * HALF + s0, h * HALF + s0 + QUARTER)
                 nc.vector.quantize_mx(
@@ -164,11 +146,11 @@ def tile_list_tgn_ema_kernel(
             words = u_dram[g].rearrange("a p n i -> p a (n i)")[:, :, 4 * n0 : 4 * (n0 + width)].bitcast(I32)
             nc.sync.dma_start(out=u_codes[g][:, :, n0 : n0 + width], in_=words)
 
-        def prep_w(c, g, lend=None):
-            raw, n0 = w_raw[c * P // CHUNK, g], c * P % CHUNK
-            grouped = staging([P, PASSES, P, PACK], BF16, "w_grouped", lend)
+        def prep_w(c, g, shared=None):
+            ch, n0 = divmod(c * P, CHUNK)
+            grouped = staging([P, PASSES, P, PACK], BF16, "w_grouped", shared)
             for a in range(PASSES):
-                interleave(grouped[:, a, :, :], raw[:, a, :, n0 : n0 + P])
+                interleave(grouped[:, a, :, :], w_raw[ch, g][:, a, :, n0 : n0 + P], nc.scalar.copy)
             codes = keep.tile([P, PASSES * P], U32, name=f"w_codes{c}_{g}", align_bytes=64)
             sc = keep.tile([P, PASSES * P], U8, name=f"w_sc{c}_{g}", align_bytes=64)
             nc.vector.quantize_mx(
@@ -179,63 +161,54 @@ def tile_list_tgn_ema_kernel(
         h_tiles = {}
 
         def load_h(c):
-            h_tiles[c] = ring.tile([P, T], F32, name="h_tile", tag="wide", bufs=4)
+            h_tiles[c] = ring.tile([P, T], F32, name="h_tile", tag="wide", bufs=WIDE)
             nc.sync.dma_start(out=h_tiles[c][:], in_=hT[c * P : (c + 1) * P, :])
 
-        wgo_sb = keep.tile([P, J], F32, name="wgo_sb")
-
-        def sums(c, j0, width, g, acc):
+        def multiply(c, h, pair):
             cols = slice(c * P, (c + 1) * P)
-            h, t0 = divmod(j0, HALF)
-            run = width if width == HALF else P
-            for a in range(PASSES):
-                for r0 in range(0, width, run):
-                    v0 = t0 + r0
+            events = slice(h * HALF, (h + 1) * HALF)
+            for g in range(2):
+                for a in range(PASSES):
                     nc.tensor.matmul_mx(
-                        out=acc[:, r0 : r0 + run],
+                        out=pair[g][:],
                         lhsT=u_codes[g][:, a, cols].bitcast(FP8X4),
                         lhsT_scale=u_sc[g][:, a, :].bitcast(U8)[:, cols],
-                        rhs=v_codes[h][:, 2 * (a * HALF + v0) : 2 * (a * HALF + v0 + run)].bitcast(FP4X4),
-                        rhs_scale=v_sc[a][:, j0 + r0 : j0 + r0 + run],
-                        start=(a == 0 and r0 == 0),
+                        rhs=v_codes[h][:, a * 2 * HALF : (a + 1) * 2 * HALF].bitcast(FP4X4),
+                        rhs_scale=v_sc[a][:, events],
+                        start=(a == 0),
                         stop=False,
                     )
-            for a in range(PASSES):
-                wc = slice(a * P, (a + 1) * P)
-                nc.tensor.matmul_mx(
-                    out=acc[:, 0:width],
-                    lhsT=w_codes[c, g][:, wc].bitcast(FP8X4),
-                    lhsT_scale=w_sc[c, g][:, wc],
-                    rhs=x_codes[:, a, j0 : j0 + width].bitcast(FP8X4),
-                    rhs_scale=x_sc[:, a, j0 : j0 + width],
-                    start=False,
-                    stop=(a == PASSES - 1),
-                )
+                for a in range(PASSES):
+                    nc.tensor.matmul_mx(
+                        out=pair[g][:],
+                        lhsT=w_codes[c, g][:, a * P : (a + 1) * P].bitcast(FP8X4),
+                        lhsT_scale=w_sc[c, g][:, a * P : (a + 1) * P],
+                        rhs=x_codes[:, a, events].bitcast(FP8X4),
+                        rhs_scale=x_sc[:, a, events],
+                        start=False,
+                        stop=(a == PASSES - 1),
+                    )
 
-        def multiply(unit, pair):
-            for g in range(2):
-                sums(*unit, g, pair[g])
-
-        def gate(c, j0, width, pair):
-            z = ring.tile([P, width], F32, name="z", bufs=3)
-            keep_gate = ring.tile([P, width], F32, name="keep_gate", bufs=3)
-            cand = ring.tile([P, width], F32, name="cand", bufs=3)
-            nc.scalar.activation(keep_gate[:], pair[0][:, 0:width], ACT.Sigmoid, bias=neg_bz[:, c : c + 1], scale=-1.0)
-            nc.scalar.activation(z[:], pair[0][:, 0:width], ACT.Sigmoid, bias=bias[0][:, c : c + 1])
-            nc.scalar.activation(cand[:], pair[1][:, 0:width], ACT.Tanh, bias=bias[1][:, c : c + 1])
-            kept = ring.tile([P, width], F32, name="kept", bufs=4)
-            nc.vector.tensor_tensor(kept[:], h_tiles[c][:].indirect(listed(j0, width)), keep_gate[:], ALU.mult)
-            new = ring.tile([P, width], F32, name="new", bufs=4)
+        def gate(c, h, pair):
+            z = ring.tile([P, HALF], F32, name="z", bufs=3)
+            keep_gate = ring.tile([P, HALF], F32, name="keep_gate", bufs=3)
+            cand = ring.tile([P, HALF], F32, name="cand", bufs=3)
+            nc.scalar.activation(keep_gate[:], pair[0][:], ACT.Sigmoid, bias=neg_bz[:, c : c + 1], scale=-1.0)
+            nc.scalar.activation(z[:], pair[0][:], ACT.Sigmoid, bias=bias[0][:, c : c + 1])
+            nc.scalar.activation(cand[:], pair[1][:], ACT.Tanh, bias=bias[1][:, c : c + 1])
+            kept = ring.tile([P, HALF], F32, name="kept", bufs=4)
+            nc.vector.tensor_tensor(kept[:], h_tiles[c][:].indirect(listed(h)), keep_gate[:], ALU.mult)
+            new = ring.tile([P, HALF], F32, name="new", bufs=4)
             nc.vector.tensor_tensor(new[:], z[:], cand[:], ALU.mult)
             return kept, new
 
         blocks = [slice(b * P, (b + 1) * P) for b in range(HALF // P)]
 
-        def add_direct(step, width, kept, new):
-            if step in LENT:
-                total = staging([P, width], F32, "total", step)
+        def add_direct(step, kept, new):
+            if step > 0:
+                total = staging([P, HALF], F32, "total", step)
             else:
-                total = ring.tile([P, width], F32, name="total", bufs=3)
+                total = ring.tile([P, HALF], F32, name="total", bufs=3)
             nc.vector.tensor_tensor(total[:], new[:], kept[:], ALU.add)
             return total
 
@@ -254,90 +227,86 @@ def tile_list_tgn_ema_kernel(
             nc.scalar.copy(total[:], bank[:])
             return total
 
-        def scatter(c, j0, width, total):
+        def scatter(c, h, total):
             window = windows[c % WINDOWS]
-            target = window[:].indirect(listed(j0, width))
-            nc.vector.tensor_tensor(target, total[:], wgo_sb[:, j0 : j0 + width], ALU.mult)
-            if j0 + width == J:
+            nc.vector.tensor_tensor(window[:].indirect(listed(h)), total[:], wgo_sb[:, h * HALF : (h + 1) * HALF], ALU.mult)
+            if h == 1:
                 nc.sync.dma_start(out=out[c * P : (c + 1) * P, :], in_=window[:])
 
         nc.sync.dma_start(out=tab_w[:], in_=tab_words[0].rearrange("p t b -> p (t b)").bitcast(I32))
-        for q in range(4):
-            load_table_scales(q)
-        x_early = [load_x_half(a, 0) for a in range(PASSES)]
-        load_bias(0)
-        load_bias(1)
-        load_event_weights()
+        for quad in range(4):
+            nc.sync.dma_start(
+                out=tab_sc[32 * quad : 32 * quad + 4 * PASSES, :], in_=tab_scales.bitcast(I32)[:, 4 * quad : 4 * quad + 4, :]
+            )
+        x_early = [load_x(a, 0) for a in range(PASSES)]
+        load_small(0, bz)
+        load_small(BN_ROW, bn)
+        load_small(WGO_ROW, wgo[0, :])
         load_w(0, 0)
         load_u(0, 0, CHUNK)
         gather_words(0)
         gather_scales()
-        lower_scales()
         load_h(0)
         load_u(1, 0, CHUNK)
         load_w(0, 1)
         load_h(1)
-        x_late = [load_x_half(a, HALF) for a in range(PASSES)]
-        load_w(1, 0)
-        load_w(1, 1)
-        load_u(0, CHUNK, CHUNK)
-        load_u(1, CHUNK, CHUNK)
+        x_late = [load_x(a, 1) for a in range(PASSES)]
+        for g in range(2):
+            load_w(1, g)
+        for g in range(2):
+            load_u(g, CHUNK, CHUNK)
         load_h(2)
         for a in range(PASSES):
             prep_x(a, 0, x_early[a])
-        turn_bias()
+        turn_small()
         spread_event_weights()
-        prep_w(0, 0)
-        prep_w(0, 1)
-        prep_w(1, 0)
-        prep_w(1, 1)
+        for c in range(2):
+            for g in range(2):
+                prep_w(c, g)
         gather_words(1)
-        for win in windows:
-            nc.vector.memset(win[:], 0.0)
+        for window in windows:
+            nc.vector.memset(window[:], 0.0)
 
-        units = [(0, 0, HALF), (1, 0, HALF), (0, HALF, HALF), (1, HALF, HALF)]
-        units = units + [(c, h * HALF, HALF) for c in range(2, TILES) for h in range(2)]
-        DIRECT = 3
-        LENT = (1, 2)
+        units = [(0, 0), (1, 0), (0, 1), (1, 1)] + [(c, h) for c in range(2, TILES) for h in range(2)]
 
-        def extra(i):
-            if i == 1:
+        def ahead(step):
+            if step == 1:
                 prep_x(0, 1, x_late[0])
-                prep_x(1, 1, x_late[1], 1, nc.vector.tensor_copy)
-            if i == 2:
+                prep_x(1, 1, x_late[1], step)
+            if step == 2:
                 prep_w(2, 0)
-                prep_w(2, 1, 2)
+                prep_w(2, 1, step)
                 load_h(3)
-                load_w(2, 0)
-                load_w(2, 1)
-                load_u(0, HALF, HALF)
-                load_u(1, HALF, HALF)
-            if i == 3:
+                for g in range(2):
+                    load_w(2, g)
+                for g in range(2):
+                    load_u(g, 2 * CHUNK, 2 * CHUNK)
+            if step == 3:
                 load_h(4)
                 load_h(5)
-                load_w(3, 0)
-                load_w(3, 1)
-            if 3 <= i < 13:
-                prep_w((i + 3) // 2, (i + 1) % 2)
-            if i == 5:
-                load_h(6)
-            if i == 7:
-                load_h(7)
+                for g in range(2):
+                    load_w(3, g)
+            c, g = divmod(step + 3, 2)
+            if 3 <= c < TILES:
+                prep_w(c, g)
+            c, even = divmod(step - 1, 2)
+            if even == 0 and 6 <= c + WIDE < TILES:
+                load_h(c + WIDE)
 
         def pair_of(step):
             return banks[2 * (step % 4) : 2 * (step % 4) + 2]
 
         parts, turned = {}, {}
-        multiply(units[0], pair_of(0))
+        multiply(*units[0], pair_of(0))
         for step in range(len(units) + 2):
             pair = pair_of(step)
             if step < len(units):
                 parts[step] = gate(*units[step], pair)
-            extra(step)
+            ahead(step)
             if step + 1 < len(units):
-                multiply(units[step + 1], pair_of(step + 1))
+                multiply(*units[step + 1], pair_of(step + 1))
             if step < DIRECT:
-                scatter(*units[step], add_direct(step, units[step][2], *parts[step]))
+                scatter(*units[step], add_direct(step, *parts[step]))
             if step - 2 >= DIRECT:
                 total = turn_back(turned[step - 2], pair[0])
             if DIRECT <= step - 1 < len(units):

@@ -53,6 +53,9 @@ def tile_list_tgn_ema_kernel(
         nc.vector.memset(tab_sc[:], 0)
         v_sc = [keep.tile([P, J], U8, name=f"v_sc{a}", align_bytes=64) for a in range(PASSES)]
         nc.vector.memset(v_sc[1][:].bitcast(I32), 0)
+        warm = keep.tile([P, 8], F32, name="warm")
+        nc.vector.memset(warm[:, 0:4], 0.0)
+        nc.scalar.activation(warm[:, 4:8], warm[:, 0:4], ACT.Sigmoid)
         for sc_tile, scales in zip(u_sc, (uz_scales, un_scales)):
             nc.vector.memset(sc_tile[:], 0)
             for quad in range(4):
@@ -140,17 +143,25 @@ def tile_list_tgn_ema_kernel(
             raw = ring.tile([P, PASSES, PACK, CHUNK], F32, name="w_raw", tag="raw", bufs=RAW)
             for a in range(PASSES):
                 load_rows(raw[:, a, :, :], w_dram[g][a * KP : (a + 1) * KP, ch * CHUNK : (ch + 1) * CHUNK])
-            w_raw[ch, g] = raw
+            for t in range(CHUNK // P):
+                w_raw[ch * CHUNK // P + t, g] = raw[:, :, :, t * P : (t + 1) * P]
+
+        def load_w_by_tile(ch, g):
+            raw = ring.tile([P, CHUNK // P, PASSES, PACK, P], F32, name="w_raw", tag="raw", bufs=RAW)
+            for t in range(CHUNK // P):
+                c = ch * CHUNK // P + t
+                for a in range(PASSES):
+                    load_rows(raw[:, t, a, :, :], w_dram[g][a * KP : (a + 1) * KP, c * P : (c + 1) * P])
+                w_raw[c, g] = raw[:, t]
 
         def load_u(g, n0, width):
             words = u_dram[g].rearrange("a p n i -> p a (n i)")[:, :, 4 * n0 : 4 * (n0 + width)].bitcast(I32)
             nc.sync.dma_start(out=u_codes[g][:, :, n0 : n0 + width], in_=words)
 
-        def prep_w(c, g, shared=None):
-            ch, n0 = divmod(c * P, CHUNK)
+        def prep_w(c, g, shared=None, copy=nc.scalar.copy):
             grouped = staging([P, PASSES, P, PACK], BF16, "w_grouped", shared)
             for a in range(PASSES):
-                interleave(grouped[:, a, :, :], w_raw[ch, g][:, a, :, n0 : n0 + P], nc.scalar.copy)
+                interleave(grouped[:, a, :, :], w_raw[c, g][:, a, :, :], copy)
             codes = keep.tile([P, PASSES * P], U32, name=f"w_codes{c}_{g}", align_bytes=64)
             sc = keep.tile([P, PASSES * P], U8, name=f"w_sc{c}_{g}", align_bytes=64)
             nc.vector.quantize_mx(
@@ -248,7 +259,7 @@ def tile_list_tgn_ema_kernel(
         gather_scales()
         load_h(0)
         load_u(1, 0, CHUNK)
-        load_w(0, 1)
+        load_w_by_tile(0, 1)
         load_h(1)
         x_late = [load_x(a, 1) for a in range(PASSES)]
         for g in range(2):
@@ -256,13 +267,14 @@ def tile_list_tgn_ema_kernel(
         for g in range(2):
             load_u(g, CHUNK, CHUNK)
         load_h(2)
-        for a in range(PASSES):
-            prep_x(a, 0, x_early[a])
+        prep_x(0, 0, x_early[0])
+        prep_x(1, 0, x_early[1], None, nc.vector.tensor_copy)
         turn_small()
         spread_event_weights()
-        for c in range(2):
-            for g in range(2):
-                prep_w(c, g)
+        prep_w(0, 0)
+        prep_w(0, 1, None, nc.vector.tensor_copy)
+        prep_w(1, 0)
+        prep_w(1, 1)
         gather_words(1)
         for window in windows:
             nc.vector.memset(window[:], 0.0)
@@ -272,7 +284,7 @@ def tile_list_tgn_ema_kernel(
         def ahead(step):
             if step == 1:
                 prep_x(0, 1, x_late[0])
-                prep_x(1, 1, x_late[1], step)
+                prep_x(1, 1, x_late[1], step, nc.vector.tensor_copy)
             if step == 2:
                 prep_w(2, 0)
                 prep_w(2, 1, step)
@@ -289,9 +301,8 @@ def tile_list_tgn_ema_kernel(
             c, g = divmod(step + 3, 2)
             if 3 <= c < TILES:
                 prep_w(c, g)
-            c, even = divmod(step - 1, 2)
-            if even == 0 and 6 <= c + WIDE < TILES:
-                load_h(c + WIDE)
+            if step in (5, 7):
+                load_h(step // 2 + WIDE)
 
         def pair_of(step):
             return banks[2 * (step % 4) : 2 * (step % 4) + 2]

@@ -29,6 +29,9 @@ WINDOWS = 3
 RAW = 5
 WIDE = 4
 DIRECT = 3
+FIRST_RATIO = 10
+FLOOR = 24.0
+PARKED = 4
 BN_ROW, WGO_ROW = 32, 64
 
 
@@ -68,8 +71,9 @@ def tile_list_tgn_ema_kernel(
         make_identity(nc, ident[:])
         tab_w = ring.tile([P, T], I32, name="tab_w", tag="wide", bufs=WIDE)
         small_cols = keep.tile([P, WGO_ROW + J // P], F32, name="small_cols")
-        bias = [small_cols[:, 0:TILES], small_cols[:, BN_ROW : BN_ROW + TILES]]
-        neg_bz = keep.tile([P, TILES], F32, name="neg_bz")
+        bn_cols = small_cols[:, BN_ROW : BN_ROW + TILES]
+        signed_bz = keep.tile([P, 2 * TILES], F32, name="signed_bz", tag="gate_bias")
+        raised_bz = keep.tile([P, TILES], F32, name="raised_bz")
         wgo_sb = keep.tile([P, J], F32, name="wgo_sb")
 
         def load_small(row, vector):
@@ -78,7 +82,9 @@ def tile_list_tgn_ema_kernel(
         def turn_small():
             nc.tensor.transpose(banks[7][:, 0:P], small_rows[:], ident[:])
             nc.scalar.copy(small_cols[:], banks[7][:, 0 : WGO_ROW + J // P])
-            nc.scalar.activation(neg_bz[:], banks[7][:, 0:TILES], ACT.Copy, scale=-1.0)
+            nc.scalar.activation(signed_bz[:, 0:TILES], banks[7][:, 0:TILES], ACT.Copy, scale=-1.0)
+            nc.scalar.copy(signed_bz[:, TILES:], banks[7][:, 0:TILES])
+            nc.scalar.activation(raised_bz[:], banks[7][:, 0:TILES], ACT.Copy, bias=FLOOR)
 
         def spread_event_weights():
             for h in range(2):
@@ -175,13 +181,13 @@ def tile_list_tgn_ema_kernel(
             h_tiles[c] = ring.tile([P, T], F32, name="h_tile", tag="wide", bufs=WIDE)
             nc.sync.dma_start(out=h_tiles[c][:], in_=hT[c * P : (c + 1) * P, :])
 
-        def multiply(c, h, pair):
+        def multiply(c, h, gate_banks):
             cols = slice(c * P, (c + 1) * P)
             events = slice(h * HALF, (h + 1) * HALF)
-            for g in range(2):
+            for g, bank in gate_banks:
                 for a in range(PASSES):
                     nc.tensor.matmul_mx(
-                        out=pair[g][:],
+                        out=bank[:],
                         lhsT=u_codes[g][:, a, cols].bitcast(FP8X4),
                         lhsT_scale=u_sc[g][:, a, :].bitcast(U8)[:, cols],
                         rhs=v_codes[h][:, a * 2 * HALF : (a + 1) * 2 * HALF].bitcast(FP4X4),
@@ -191,7 +197,7 @@ def tile_list_tgn_ema_kernel(
                     )
                 for a in range(PASSES):
                     nc.tensor.matmul_mx(
-                        out=pair[g][:],
+                        out=bank[:],
                         lhsT=w_codes[c, g][:, a * P : (a + 1) * P].bitcast(FP8X4),
                         lhsT_scale=w_sc[c, g][:, a * P : (a + 1) * P],
                         rhs=x_codes[:, a, events].bitcast(FP8X4),
@@ -200,13 +206,50 @@ def tile_list_tgn_ema_kernel(
                         stop=(a == PASSES - 1),
                     )
 
-        def gate(c, h, pair):
+        parked = []
+
+        def parked_part(kind, unit):
+            if not parked:
+                parked.extend(ring.tile([P, PARKED * HALF], F32, name="parked", tag="raw", bufs=RAW) for b in range(3))
+            n = unit - FIRST_RATIO
+            tile, at = (parked[kind], n) if n < PARKED else (parked[2], 2 * kind + n - PARKED)
+            return tile[:, at * HALF : (at + 1) * HALF]
+
+        def held(unit):
+            return parked_part(0, unit)
+
+        def ratio(unit):
+            return parked_part(1, unit)
+
+        def late_z(unit):
+            return ratio(unit + 1 if unit + 1 < len(units) else FIRST_RATIO)
+
+        def hold_argument(unit, bank):
+            c, h = units[unit]
+            multiply(c, h, [(0, bank)])
+            nc.scalar.activation(held(unit), bank[:], ACT.Relu, bias=raised_bz[:, c : c + 1])
+
+        def floor_column(name, value):
+            column = keep.tile([P, TILES], F32, name=name, tag="gate_bias")
+            nc.scalar.activation(column[:], raised_bz[:], ACT.Copy, scale=0.0, bias=value)
+            return column[:, 0:1]
+
+        def gate_ratio(unit, pair):
+            c, h = units[unit]
+            cand = ring.tile([P, HALF], F32, name="cand", bufs=3)
+            nc.scalar.activation(cand[:], pair[1][:], ACT.Tanh, bias=bn_cols[:, c : c + 1])
+            kept = ring.tile([P, HALF], F32, name="kept", bufs=4)
+            nc.vector.tensor_tensor(kept[:], h_tiles[c][:].indirect(listed(h)), ratio(unit), ALU.mult)
+            return kept, cand
+
+        def gate_product(unit, pair):
+            c, h = units[unit]
             z = ring.tile([P, HALF], F32, name="z", bufs=3)
             keep_gate = ring.tile([P, HALF], F32, name="keep_gate", bufs=3)
             cand = ring.tile([P, HALF], F32, name="cand", bufs=3)
-            nc.scalar.activation(keep_gate[:], pair[0][:], ACT.Sigmoid, bias=neg_bz[:, c : c + 1], scale=-1.0)
-            nc.scalar.activation(z[:], pair[0][:], ACT.Sigmoid, bias=bias[0][:, c : c + 1])
-            nc.scalar.activation(cand[:], pair[1][:], ACT.Tanh, bias=bias[1][:, c : c + 1])
+            nc.scalar.activation(keep_gate[:], pair[0][:], ACT.Sigmoid, bias=signed_bz[:, c : c + 1], scale=-1.0)
+            nc.scalar.activation(z[:], pair[0][:], ACT.Sigmoid, bias=signed_bz[:, TILES + c : TILES + c + 1])
+            nc.scalar.activation(cand[:], pair[1][:], ACT.Tanh, bias=bn_cols[:, c : c + 1])
             kept = ring.tile([P, HALF], F32, name="kept", bufs=4)
             nc.vector.tensor_tensor(kept[:], h_tiles[c][:].indirect(listed(h)), keep_gate[:], ALU.mult)
             new = ring.tile([P, HALF], F32, name="new", bufs=4)
@@ -223,12 +266,17 @@ def tile_list_tgn_ema_kernel(
             nc.vector.tensor_tensor(total[:], new[:], kept[:], ALU.add)
             return total
 
-        def add_turned(kept, new, bank):
+        def add_turned(unit, kept, new, bank):
             for blk in blocks:
                 nc.tensor.matmul(bank[:, blk], kept[:, blk], ident[:], start=True, stop=False, is_transpose=True)
                 nc.tensor.matmul(bank[:, blk], new[:, blk], ident[:], start=False, stop=True, is_transpose=True)
             by_event = ring.tile([P, HALF], F32, name="by_event", bufs=3)
-            nc.scalar.copy(by_event[:], bank[:])
+            if unit < FIRST_RATIO:
+                nc.scalar.copy(by_event[:], bank[:])
+            else:
+                for b, blk in enumerate(blocks):
+                    col = WGO_ROW + units[unit][1] * len(blocks) + b
+                    nc.scalar.activation(by_event[:, blk], bank[:, blk], ACT.Copy, scale=small_cols[:, col : col + 1])
             return by_event
 
         def turn_back(by_event, bank):
@@ -238,9 +286,11 @@ def tile_list_tgn_ema_kernel(
             nc.scalar.copy(total[:], bank[:])
             return total
 
-        def scatter(c, h, total):
+        def scatter(unit, total):
+            c, h = units[unit]
             window = windows[c % WINDOWS]
-            nc.vector.tensor_tensor(window[:].indirect(listed(h)), total[:], wgo_sb[:, h * HALF : (h + 1) * HALF], ALU.mult)
+            factor = wgo_sb[:, h * HALF : (h + 1) * HALF] if unit < FIRST_RATIO else late_z(unit)
+            nc.vector.tensor_tensor(window[:].indirect(listed(h)), total[:], factor, ALU.mult)
             if h == 1:
                 nc.sync.dma_start(out=out[c * P : (c + 1) * P, :], in_=window[:])
 
@@ -281,6 +331,9 @@ def tile_list_tgn_ema_kernel(
 
         units = [(0, 0), (1, 0), (0, 1), (1, 1)] + [(c, h) for c in range(2, TILES) for h in range(2)]
 
+        ratio_tiles = range(FIRST_RATIO // 2, TILES)
+        ratio_units = range(FIRST_RATIO, len(units))
+
         def ahead(step):
             if step == 1:
                 prep_x(0, 1, x_late[0])
@@ -299,8 +352,10 @@ def tile_list_tgn_ema_kernel(
                 for g in range(2):
                     load_w(3, g)
             c, g = divmod(step + 3, 2)
-            if 3 <= c < TILES:
+            if 3 <= c < TILES and (c not in ratio_tiles or g == 1):
                 prep_w(c, g)
+            if step in ratio_tiles:
+                prep_w(step, 0)
             if step in (5, 7):
                 load_h(step // 2 + WIDE)
 
@@ -308,19 +363,37 @@ def tile_list_tgn_ema_kernel(
             return banks[2 * (step % 4) : 2 * (step % 4) + 2]
 
         parts, turned = {}, {}
-        multiply(*units[0], pair_of(0))
+        multiply(*units[0], enumerate(pair_of(0)))
         for step in range(len(units) + 2):
             pair = pair_of(step)
-            if step < len(units):
-                parts[step] = gate(*units[step], pair)
+            if step < FIRST_RATIO:
+                parts[step] = gate_product(step, pair)
+            elif step < len(units):
+                parts[step] = gate_ratio(step, pair)
+            if step - 1 in ratio_units:
+                nc.scalar.activation(late_z(step - 1), held(step - 1), ACT.Sigmoid, bias=neg_floor)
             ahead(step)
-            if step + 1 < len(units):
-                multiply(*units[step + 1], pair_of(step + 1))
+            if step + 1 < FIRST_RATIO:
+                multiply(*units[step + 1], enumerate(pair_of(step + 1)))
+            elif step + 1 < len(units):
+                multiply(*units[step + 1], [(1, pair_of(step + 1)[1])])
+            if step - 2 in ratio_tiles:
+                for h in range(2):
+                    hold_argument(2 * (step - 2) + h, pair_of(step + 2)[h])
+            if step == FIRST_RATIO - 1:
+                floor = floor_column("floor", FLOOR)
+            if step in (FIRST_RATIO - 1, FIRST_RATIO):
+                share = len(ratio_units) // 2
+                first = (step - FIRST_RATIO + 1) * share
+                for unit in ratio_units[first : first + share]:
+                    nc.scalar.activation(ratio(unit), held(unit), ACT.Exp, bias=floor, scale=-1.0)
+            if step == FIRST_RATIO:
+                neg_floor = floor_column("neg_floor", -FLOOR)
             if step < DIRECT:
-                scatter(*units[step], add_direct(step, *parts[step]))
+                scatter(step, add_direct(step, *parts[step]))
             if step - 2 >= DIRECT:
                 total = turn_back(turned[step - 2], pair[0])
             if DIRECT <= step - 1 < len(units):
-                turned[step - 1] = add_turned(*parts[step - 1], pair[1])
+                turned[step - 1] = add_turned(step - 1, *parts[step - 1], pair[1])
             if step - 2 >= DIRECT:
-                scatter(*units[step - 2], total)
+                scatter(step - 2, total)

@@ -32,7 +32,10 @@ DIRECT = 3
 FIRST_RATIO = 10
 FLOOR = 24.0
 PARKED = 4
-BN_ROW, WGO_ROW = 32, 64
+BN_ROW = 32
+GROUPED = 4
+GATES = 3
+TERMS = 4
 
 
 def tile_list_tgn_ema_kernel(
@@ -51,56 +54,64 @@ def tile_list_tgn_ema_kernel(
         def listed(h):
             return offsets[:, h * HALF // 16 : (h + 1) * HALF // 16]
 
-        tab_sc = keep.tile([P, T // 4], I32, name="tab_sc", align_bytes=64)
+        tab_sc = keep.tile([P, PASSES, T // 4], I32, name="tab_sc", align_bytes=64)
         u_sc = [keep.tile([P, PASSES, N // 4], I32, name=f"u_sc{g}", align_bytes=64) for g in range(2)]
-        nc.vector.memset(tab_sc[:], 0)
-        v_sc = [keep.tile([P, J], U8, name=f"v_sc{a}", align_bytes=64) for a in range(PASSES)]
-        nc.vector.memset(v_sc[1][:].bitcast(I32), 0)
+        for sc_tile in [tab_sc] + u_sc:
+            nc.vector.memset(sc_tile[:], 0)
         warm = keep.tile([P, 8], F32, name="warm")
         nc.vector.memset(warm[:, 0:4], 0.0)
         nc.scalar.activation(warm[:, 4:8], warm[:, 0:4], ACT.Sigmoid)
-        for sc_tile, scales in zip(u_sc, (uz_scales, un_scales)):
-            nc.vector.memset(sc_tile[:], 0)
-            for quad in range(4):
-                rows = scales.bitcast(I32)[:, 4 * quad : 4 * quad + 4, :]
-                nc.gpsimd.dma_start(out=sc_tile[32 * quad : 32 * quad + 4, :, :], in_=rows.rearrange("a r n -> r a n"))
 
-        small_rows = keep.tile([P, P], F32, name="small_rows")
-        nc.vector.memset(small_rows[:], 0.0)
+        bias_rows = keep.tile([P, P], F32, name="bias_rows")
+        nc.vector.memset(bias_rows[:], 0.0)
+        wgo_rows = keep.tile([P, P], F32, name="wgo_rows")
+        nc.vector.memset(wgo_rows[:], 0.0)
+        wgo_cols = keep.tile([P, J // P], F32, name="wgo_cols")
         ident = keep.tile([P, P], F32, name="ident")
         make_identity(nc, ident[:])
         tab_w = ring.tile([P, T], I32, name="tab_w", tag="wide", bufs=WIDE)
-        small_cols = keep.tile([P, WGO_ROW + J // P], F32, name="small_cols")
-        bn_cols = small_cols[:, BN_ROW : BN_ROW + TILES]
+        bn_cols = keep.tile([P, TILES], F32, name="bn_cols")
         signed_bz = keep.tile([P, 2 * TILES], F32, name="signed_bz", tag="gate_bias")
         raised_bz = keep.tile([P, TILES], F32, name="raised_bz")
         wgo_sb = keep.tile([P, J], F32, name="wgo_sb")
 
-        def load_small(row, vector):
-            nc.sync.dma_start(out=small_rows[row : row + TILES, :], in_=vector.rearrange("(c p) -> c p", p=P))
+        def load_vector(rows, row, vector):
+            nc.sync.dma_start(out=rows[row : row + TILES, :], in_=vector.rearrange("(c p) -> c p", p=P))
 
-        def turn_small():
-            nc.tensor.transpose(banks[7][:, 0:P], small_rows[:], ident[:])
-            nc.scalar.copy(small_cols[:], banks[7][:, 0 : WGO_ROW + J // P])
+        def load_scales(sc_tile, scales):
+            for quad in range(4):
+                rows = scales.bitcast(I32)[:, 4 * quad : 4 * quad + 4, :]
+                nc.sync.dma_start(out=sc_tile[32 * quad : 32 * quad + 4, :, :], in_=rows.rearrange("a r n -> r a n"))
+
+        def turn_biases():
+            nc.tensor.transpose(banks[7][:, 0:P], bias_rows[:], ident[:])
+            nc.scalar.copy(bn_cols[:], banks[7][:, BN_ROW : BN_ROW + TILES])
             nc.scalar.activation(signed_bz[:, 0:TILES], banks[7][:, 0:TILES], ACT.Copy, scale=-1.0)
             nc.scalar.copy(signed_bz[:, TILES:], banks[7][:, 0:TILES])
             nc.scalar.activation(raised_bz[:], banks[7][:, 0:TILES], ACT.Copy, bias=FLOOR)
 
         def spread_event_weights():
+            nc.tensor.transpose(banks[4][:, 0:P], wgo_rows[:], ident[:])
+            nc.scalar.copy(wgo_cols[:], banks[4][:, 0 : J // P])
             for h in range(2):
                 for b in range(HALF // P):
-                    col = WGO_ROW + h * (HALF // P) + b
+                    col = h * (HALF // P) + b
                     nc.tensor.transpose(
-                        banks[5 + h][:, b * P : (b + 1) * P], small_cols[:, col : col + 1].to_broadcast([P, P]), ident[:]
+                        banks[5 + h][:, b * P : (b + 1) * P], wgo_cols[:, col : col + 1].to_broadcast([P, P]), ident[:]
                     )
                 nc.scalar.copy(wgo_sb[:, h * HALF : (h + 1) * HALF], banks[5 + h][:])
 
         windows = [keep.tile([P, T], F32, name=f"window{b}") for b in range(WINDOWS)]
 
-        v_codes = {}
+        def staging(shape, dtype, name, shared):
+            if shared is None:
+                return ring.tile(shape, dtype, name=name, tag="grouped", bufs=GROUPED, align_bytes=64)
+            return ring.tile(shape, dtype, name=name, tag=f"shared{shared}", bufs=1, align_bytes=64)
 
-        def gather_words(h):
-            pairs = keep.tile([P, HALF], U32, name=f"v_pairs{h}", align_bytes=64)
+        v_codes, v_sc = {}, {}
+
+        def gather_words(h, shared):
+            pairs = staging([P, HALF], U32, "v_pairs", shared)
             nc.vector.tensor_copy(pairs[:], tab_w[:].bitcast(U32).indirect(listed(h)))
             v_codes[h] = keep.tile([P, PASSES * 2 * HALF], U8, name=f"v_codes{h}", align_bytes=64)
             nc.vector.tensor_copy(
@@ -108,20 +119,16 @@ def tile_list_tgn_ema_kernel(
                 pairs[:].bitcast(U16).rearrange("p (j a) -> p a j", a=PASSES),
             )
 
-        def gather_scales():
-            nc.vector.tensor_copy(v_sc[0][:], tab_sc[:].bitcast(U8).indirect(offsets[:]))
-            nc.sync.dma_start(out=v_sc[1][0:112, :].bitcast(I32), in_=v_sc[0][4:116, :].bitcast(I32))
+        def gather_scales(h, shared):
+            for a in range(PASSES):
+                v_sc[h, a] = staging([P, HALF], U8, "v_sc", shared[a])
+                nc.vector.tensor_copy(v_sc[h, a][:], tab_sc[:, a, :].bitcast(U8).indirect(listed(h)))
 
         def load_rows(raw, rows):
             nc.sync.dma_start(out=raw, in_=rows.rearrange("(p i) w -> p i w", i=PACK))
 
         def interleave(grouped, raw, copy):
             copy(out=grouped.rearrange("p (c e) i -> p c i e", e=4), in_=raw.rearrange("p i (c e) -> p c i e", e=4))
-
-        def staging(shape, dtype, name, shared):
-            if shared is None:
-                return ring.tile(shape, dtype, name=name, tag="grouped", bufs=4, align_bytes=64)
-            return ring.tile(shape, dtype, name=name, tag=f"shared{shared}", bufs=1, align_bytes=64)
 
         x_codes = keep.tile([P, PASSES, J], U32, name="x_codes", align_bytes=64)
         x_sc = keep.tile([P, PASSES, J], U8, name="x_sc", align_bytes=64)
@@ -131,8 +138,8 @@ def tile_list_tgn_ema_kernel(
             load_rows(raw[:], x[a * KP : (a + 1) * KP, h * HALF : (h + 1) * HALF])
             return raw
 
-        def prep_x(a, h, raw, shared=None, copy=nc.scalar.copy):
-            for s0 in range(0, HALF, QUARTER):
+        def prep_x(a, h, raw, shared=None, copies=(nc.scalar.copy, nc.scalar.copy)):
+            for s0, copy in zip(range(0, HALF, QUARTER), copies):
                 grouped = staging([P, QUARTER, PACK], BF16, "x_grouped", shared if s0 + QUARTER == HALF else None)
                 interleave(grouped[:], raw[:, :, s0 : s0 + QUARTER], copy)
                 cols = slice(h * HALF + s0, h * HALF + s0 + QUARTER)
@@ -191,7 +198,7 @@ def tile_list_tgn_ema_kernel(
                         lhsT=u_codes[g][:, a, cols].bitcast(FP8X4),
                         lhsT_scale=u_sc[g][:, a, :].bitcast(U8)[:, cols],
                         rhs=v_codes[h][:, a * 2 * HALF : (a + 1) * 2 * HALF].bitcast(FP4X4),
-                        rhs_scale=v_sc[a][:, events],
+                        rhs_scale=v_sc[h, a][:],
                         start=(a == 0),
                         stop=False,
                     )
@@ -236,23 +243,23 @@ def tile_list_tgn_ema_kernel(
 
         def gate_ratio(unit, pair):
             c, h = units[unit]
-            cand = ring.tile([P, HALF], F32, name="cand", bufs=3)
+            cand = ring.tile([P, HALF], F32, name="cand", bufs=GATES)
             nc.scalar.activation(cand[:], pair[1][:], ACT.Tanh, bias=bn_cols[:, c : c + 1])
-            kept = ring.tile([P, HALF], F32, name="kept", bufs=4)
+            kept = ring.tile([P, HALF], F32, name="kept", bufs=TERMS)
             nc.vector.tensor_tensor(kept[:], h_tiles[c][:].indirect(listed(h)), ratio(unit), ALU.mult)
             return kept, cand
 
         def gate_product(unit, pair):
             c, h = units[unit]
-            z = ring.tile([P, HALF], F32, name="z", bufs=3)
-            keep_gate = ring.tile([P, HALF], F32, name="keep_gate", bufs=3)
-            cand = ring.tile([P, HALF], F32, name="cand", bufs=3)
+            z = ring.tile([P, HALF], F32, name="z", bufs=GATES)
+            keep_gate = ring.tile([P, HALF], F32, name="keep_gate", bufs=GATES)
+            cand = ring.tile([P, HALF], F32, name="cand", bufs=GATES)
             nc.scalar.activation(keep_gate[:], pair[0][:], ACT.Sigmoid, bias=signed_bz[:, c : c + 1], scale=-1.0)
             nc.scalar.activation(z[:], pair[0][:], ACT.Sigmoid, bias=signed_bz[:, TILES + c : TILES + c + 1])
             nc.scalar.activation(cand[:], pair[1][:], ACT.Tanh, bias=bn_cols[:, c : c + 1])
-            kept = ring.tile([P, HALF], F32, name="kept", bufs=4)
+            kept = ring.tile([P, HALF], F32, name="kept", bufs=TERMS)
             nc.vector.tensor_tensor(kept[:], h_tiles[c][:].indirect(listed(h)), keep_gate[:], ALU.mult)
-            new = ring.tile([P, HALF], F32, name="new", bufs=4)
+            new = ring.tile([P, HALF], F32, name="new", bufs=TERMS)
             nc.vector.tensor_tensor(new[:], z[:], cand[:], ALU.mult)
             return kept, new
 
@@ -262,7 +269,7 @@ def tile_list_tgn_ema_kernel(
             if step > 0:
                 total = staging([P, HALF], F32, "total", step)
             else:
-                total = ring.tile([P, HALF], F32, name="total", bufs=3)
+                total = ring.tile([P, HALF], F32, name="total", bufs=GATES)
             nc.vector.tensor_tensor(total[:], new[:], kept[:], ALU.add)
             return total
 
@@ -270,19 +277,19 @@ def tile_list_tgn_ema_kernel(
             for blk in blocks:
                 nc.tensor.matmul(bank[:, blk], kept[:, blk], ident[:], start=True, stop=False, is_transpose=True)
                 nc.tensor.matmul(bank[:, blk], new[:, blk], ident[:], start=False, stop=True, is_transpose=True)
-            by_event = ring.tile([P, HALF], F32, name="by_event", bufs=3)
+            by_event = ring.tile([P, HALF], F32, name="by_event", bufs=GATES)
             if unit < FIRST_RATIO:
                 nc.scalar.copy(by_event[:], bank[:])
             else:
                 for b, blk in enumerate(blocks):
-                    col = WGO_ROW + units[unit][1] * len(blocks) + b
-                    nc.scalar.activation(by_event[:, blk], bank[:, blk], ACT.Copy, scale=small_cols[:, col : col + 1])
+                    col = units[unit][1] * len(blocks) + b
+                    nc.scalar.activation(by_event[:, blk], bank[:, blk], ACT.Copy, scale=wgo_cols[:, col : col + 1])
             return by_event
 
         def turn_back(by_event, bank):
             for blk in blocks:
                 nc.tensor.transpose(bank[:, blk], by_event[:, blk], ident[:])
-            total = ring.tile([P, HALF], F32, name="total", bufs=3)
+            total = ring.tile([P, HALF], F32, name="total", bufs=GATES)
             nc.scalar.copy(total[:], bank[:])
             return total
 
@@ -295,19 +302,18 @@ def tile_list_tgn_ema_kernel(
                 nc.sync.dma_start(out=out[c * P : (c + 1) * P, :], in_=window[:])
 
         nc.sync.dma_start(out=tab_w[:], in_=tab_words[0].rearrange("p t b -> p (t b)").bitcast(I32))
-        for quad in range(4):
-            nc.sync.dma_start(
-                out=tab_sc[32 * quad : 32 * quad + 4 * PASSES, :], in_=tab_scales.bitcast(I32)[:, 4 * quad : 4 * quad + 4, :]
-            )
+        load_scales(tab_sc, tab_scales)
         x_early = [load_x(a, 0) for a in range(PASSES)]
-        load_small(0, bz)
-        load_small(BN_ROW, bn)
-        load_small(WGO_ROW, wgo[0, :])
+        load_scales(u_sc[0], uz_scales)
+        load_vector(bias_rows, 0, bz)
+        load_vector(bias_rows, BN_ROW, bn)
         load_w(0, 0)
         load_u(0, 0, CHUNK)
-        gather_words(0)
-        gather_scales()
+        gather_words(0, "first_words")
+        gather_scales(0, ["first_scales0", "first_scales1"])
         load_h(0)
+        load_vector(wgo_rows, 0, wgo[0, :])
+        load_scales(u_sc[1], un_scales)
         load_u(1, 0, CHUNK)
         load_w_by_tile(0, 1)
         load_h(1)
@@ -318,18 +324,22 @@ def tile_list_tgn_ema_kernel(
             load_u(g, CHUNK, CHUNK)
         load_h(2)
         prep_x(0, 0, x_early[0])
-        prep_x(1, 0, x_early[1], None, nc.vector.tensor_copy)
-        turn_small()
+        prep_x(1, 0, x_early[1])
+        turn_biases()
+        prep_w(0, 0, "z0")
+        prep_w(0, 1, "n0", nc.vector.tensor_copy)
+        prep_w(1, 0, "z1")
         spread_event_weights()
-        prep_w(0, 0)
-        prep_w(0, 1, None, nc.vector.tensor_copy)
-        prep_w(1, 0)
         prep_w(1, 1)
-        gather_words(1)
+        gather_scales(1, ["z0", "z1"])
+        gather_words(1, "n0")
         for window in windows:
             nc.vector.memset(window[:], 0.0)
 
-        units = [(0, 0), (1, 0), (0, 1), (1, 1)] + [(c, h) for c in range(2, TILES) for h in range(2)]
+        first_tiles, last_tiles = range(2), range(TILES - 2, TILES)
+        units = [(c, h) for h in range(2) for c in first_tiles]
+        units = units + [(c, h) for c in range(2, TILES - 2) for h in range(2)]
+        units = units + [(c, h) for h in range(2) for c in last_tiles]
 
         ratio_tiles = range(FIRST_RATIO // 2, TILES)
         ratio_units = range(FIRST_RATIO, len(units))
@@ -337,7 +347,7 @@ def tile_list_tgn_ema_kernel(
         def ahead(step):
             if step == 1:
                 prep_x(0, 1, x_late[0])
-                prep_x(1, 1, x_late[1], step, nc.vector.tensor_copy)
+                prep_x(1, 1, x_late[1], step, (nc.scalar.copy, nc.vector.tensor_copy))
             if step == 2:
                 prep_w(2, 0)
                 prep_w(2, 1, step)
@@ -352,8 +362,10 @@ def tile_list_tgn_ema_kernel(
                 for g in range(2):
                     load_w(3, g)
             c, g = divmod(step + 3, 2)
-            if 3 <= c < TILES and (c not in ratio_tiles or g == 1):
+            if 3 <= c < last_tiles[-1] and (c not in ratio_tiles or g == 1):
                 prep_w(c, g)
+            if step == 2 * last_tiles[-1] - 3:
+                prep_w(last_tiles[-1], 1)
             if step in ratio_tiles:
                 prep_w(step, 0)
             if step in (5, 7):
@@ -379,7 +391,7 @@ def tile_list_tgn_ema_kernel(
                 multiply(*units[step + 1], [(1, pair_of(step + 1)[1])])
             if step - 2 in ratio_tiles:
                 for h in range(2):
-                    hold_argument(2 * (step - 2) + h, pair_of(step + 2)[h])
+                    hold_argument(units.index((step - 2, h)), pair_of(step + 2)[h])
             if step == FIRST_RATIO - 1:
                 floor = floor_column("floor", FLOOR)
             if step in (FIRST_RATIO - 1, FIRST_RATIO):

@@ -159,14 +159,6 @@ def tile_list_tgn_ema_kernel(
             for t in range(CHUNK // P):
                 w_raw[ch * CHUNK // P + t, g] = raw[:, :, :, t * P : (t + 1) * P]
 
-        def load_w_by_tile(ch, g):
-            raw = ring.tile([P, CHUNK // P, PASSES, PACK, P], F32, name="w_raw", tag="raw", bufs=RAW)
-            for t in range(CHUNK // P):
-                c = ch * CHUNK // P + t
-                for a in range(PASSES):
-                    load_rows(raw[:, t, a, :, :], w_dram[g][a * KP : (a + 1) * KP, c * P : (c + 1) * P])
-                w_raw[c, g] = raw[:, t]
-
         def load_u(g, n0, width):
             words = u_dram[g].rearrange("a p n i -> p a (n i)")[:, :, 4 * n0 : 4 * (n0 + width)].bitcast(I32)
             nc.sync.dma_start(out=u_codes[g][:, :, n0 : n0 + width], in_=words)
@@ -304,18 +296,19 @@ def tile_list_tgn_ema_kernel(
         nc.sync.dma_start(out=tab_w[:], in_=tab_words[0].rearrange("p t b -> p (t b)").bitcast(I32))
         load_scales(tab_sc, tab_scales)
         x_early = [load_x(a, 0) for a in range(PASSES)]
-        load_scales(u_sc[0], uz_scales)
         load_vector(bias_rows, 0, bz)
         load_vector(bias_rows, BN_ROW, bn)
         load_w(0, 0)
         load_u(0, 0, CHUNK)
+        load_scales(u_sc[0], uz_scales)
         gather_words(0, "first_words")
+        gather_words(1, "second_words")
         gather_scales(0, ["first_scales0", "first_scales1"])
-        load_h(0)
-        load_vector(wgo_rows, 0, wgo[0, :])
-        load_scales(u_sc[1], un_scales)
         load_u(1, 0, CHUNK)
-        load_w_by_tile(0, 1)
+        load_w(0, 1)
+        load_scales(u_sc[1], un_scales)
+        load_vector(wgo_rows, 0, wgo[0, :])
+        load_h(0)
         load_h(1)
         x_late = [load_x(a, 1) for a in range(PASSES)]
         for g in range(2):
@@ -327,12 +320,11 @@ def tile_list_tgn_ema_kernel(
         prep_x(1, 0, x_early[1])
         turn_biases()
         prep_w(0, 0, "z0")
-        prep_w(0, 1, "n0", nc.vector.tensor_copy)
         prep_w(1, 0, "z1")
+        prep_w(0, 1, None, nc.vector.tensor_copy)
         spread_event_weights()
         prep_w(1, 1)
         gather_scales(1, ["z0", "z1"])
-        gather_words(1, "n0")
         for window in windows:
             nc.vector.memset(window[:], 0.0)
 

@@ -55,8 +55,9 @@ def tile_list_tgn_ema_kernel(
             return offsets[:, h * HALF // 16 : (h + 1) * HALF // 16]
 
         tab_sc = keep.tile([P, PASSES, T // 4], I32, name="tab_sc", align_bytes=64)
-        u_sc = [keep.tile([P, PASSES, N // 4], I32, name=f"u_sc{g}", align_bytes=64) for g in range(2)]
-        for sc_tile in [tab_sc] + u_sc:
+        u_sc_first = [keep.tile([P, PASSES, CHUNK // 4], I32, name=f"u_sc_first{g}", align_bytes=64) for g in range(2)]
+        u_sc_rest = [keep.tile([P, PASSES, (N - CHUNK) // 4], I32, name=f"u_sc_rest{g}", align_bytes=64) for g in range(2)]
+        for sc_tile in [tab_sc] + u_sc_first + u_sc_rest:
             nc.vector.memset(sc_tile[:], 0)
         warm = keep.tile([P, 8], F32, name="warm")
         nc.vector.memset(warm[:, 0:4], 0.0)
@@ -71,23 +72,24 @@ def tile_list_tgn_ema_kernel(
         make_identity(nc, ident[:])
         tab_w = ring.tile([P, T], I32, name="tab_w", tag="wide", bufs=WIDE)
         bn_cols = keep.tile([P, TILES], F32, name="bn_cols")
-        signed_bz = keep.tile([P, 2 * TILES], F32, name="signed_bz", tag="gate_bias")
+        signed_bz = keep.tile([P, TILES], F32, name="signed_bz", tag="gate_bias")
+        neg_bn = keep.tile([P, TILES], F32, name="neg_bn")
         raised_bz = keep.tile([P, TILES], F32, name="raised_bz")
         wgo_sb = keep.tile([P, J], F32, name="wgo_sb")
 
         def load_vector(rows, row, vector):
             nc.sync.dma_start(out=rows[row : row + TILES, :], in_=vector.rearrange("(c p) -> c p", p=P))
 
-        def load_scales(sc_tile, scales):
+        def load_scales(sc_tile, scales, words=slice(None)):
             for quad in range(4):
-                rows = scales.bitcast(I32)[:, 4 * quad : 4 * quad + 4, :]
+                rows = scales.bitcast(I32)[:, 4 * quad : 4 * quad + 4, words]
                 nc.sync.dma_start(out=sc_tile[32 * quad : 32 * quad + 4, :, :], in_=rows.rearrange("a r n -> r a n"))
 
         def turn_biases():
             nc.tensor.transpose(banks[7][:, 0:P], bias_rows[:], ident[:])
             nc.scalar.copy(bn_cols[:], banks[7][:, BN_ROW : BN_ROW + TILES])
             nc.scalar.activation(signed_bz[:, 0:TILES], banks[7][:, 0:TILES], ACT.Copy, scale=-1.0)
-            nc.scalar.copy(signed_bz[:, TILES:], banks[7][:, 0:TILES])
+            nc.scalar.activation(neg_bn[:], banks[7][:, BN_ROW : BN_ROW + TILES], ACT.Copy, scale=-1.0)
             nc.scalar.activation(raised_bz[:], banks[7][:, 0:TILES], ACT.Copy, bias=FLOOR)
 
         def spread_event_weights():
@@ -138,10 +140,10 @@ def tile_list_tgn_ema_kernel(
             load_rows(raw[:], x[a * KP : (a + 1) * KP, h * HALF : (h + 1) * HALF])
             return raw
 
-        def prep_x(a, h, raw, shared=None, copies=(nc.scalar.copy, nc.scalar.copy)):
-            for s0, copy in zip(range(0, HALF, QUARTER), copies):
+        def prep_x(a, h, raw, shared=None):
+            for s0 in range(0, HALF, QUARTER):
                 grouped = staging([P, QUARTER, PACK], BF16, "x_grouped", shared if s0 + QUARTER == HALF else None)
-                interleave(grouped[:], raw[:, :, s0 : s0 + QUARTER], copy)
+                interleave(grouped[:], raw[:, :, s0 : s0 + QUARTER], nc.scalar.copy)
                 cols = slice(h * HALF + s0, h * HALF + s0 + QUARTER)
                 nc.vector.quantize_mx(
                     out=x_codes[:, a, cols].bitcast(FP8X4), scales=x_sc[:, a, cols], in_=grouped[:].rearrange("p w i -> p (w i)")
@@ -157,7 +159,15 @@ def tile_list_tgn_ema_kernel(
             for a in range(PASSES):
                 load_rows(raw[:, a, :, :], w_dram[g][a * KP : (a + 1) * KP, ch * CHUNK : (ch + 1) * CHUNK])
             for t in range(CHUNK // P):
-                w_raw[ch * CHUNK // P + t, g] = raw[:, :, :, t * P : (t + 1) * P]
+                w_raw[ch * CHUNK // P + t, g] = [raw[:, a, :, t * P : (t + 1) * P] for a in range(PASSES)]
+
+        def load_late_z():
+            first = N - 2 * CHUNK
+            raws = [ring.tile([P, PACK, 2 * CHUNK], F32, name="w_raw", tag="raw", bufs=RAW) for a in range(PASSES)]
+            for a in range(PASSES):
+                load_rows(raws[a][:], wz[a * KP : (a + 1) * KP, first:N])
+            for t in range(2 * CHUNK // P):
+                w_raw[first // P + t, 0] = [raw[:, :, t * P : (t + 1) * P] for raw in raws]
 
         def load_u(g, n0, width):
             words = u_dram[g].rearrange("a p n i -> p a (n i)")[:, :, 4 * n0 : 4 * (n0 + width)].bitcast(I32)
@@ -166,7 +176,7 @@ def tile_list_tgn_ema_kernel(
         def prep_w(c, g, shared=None, copy=nc.scalar.copy):
             grouped = staging([P, PASSES, P, PACK], BF16, "w_grouped", shared)
             for a in range(PASSES):
-                interleave(grouped[:, a, :, :], w_raw[c, g][:, a, :, :], copy)
+                interleave(grouped[:, a, :, :], w_raw[c, g][a], copy)
             codes = keep.tile([P, PASSES * P], U32, name=f"w_codes{c}_{g}", align_bytes=64)
             sc = keep.tile([P, PASSES * P], U8, name=f"w_sc{c}_{g}", align_bytes=64)
             nc.vector.quantize_mx(
@@ -183,12 +193,16 @@ def tile_list_tgn_ema_kernel(
         def multiply(c, h, gate_banks):
             cols = slice(c * P, (c + 1) * P)
             events = slice(h * HALF, (h + 1) * HALF)
+            if cols.stop <= CHUNK:
+                u_sc, sc_cols = u_sc_first, cols
+            else:
+                u_sc, sc_cols = u_sc_rest, slice(cols.start - CHUNK, cols.stop - CHUNK)
             for g, bank in gate_banks:
                 for a in range(PASSES):
                     nc.tensor.matmul_mx(
                         out=bank[:],
                         lhsT=u_codes[g][:, a, cols].bitcast(FP8X4),
-                        lhsT_scale=u_sc[g][:, a, :].bitcast(U8)[:, cols],
+                        lhsT_scale=u_sc[g][:, a, :].bitcast(U8)[:, sc_cols],
                         rhs=v_codes[h][:, a * 2 * HALF : (a + 1) * 2 * HALF].bitcast(FP4X4),
                         rhs_scale=v_sc[h, a][:],
                         start=(a == 0),
@@ -243,16 +257,17 @@ def tile_list_tgn_ema_kernel(
 
         def gate_product(unit, pair):
             c, h = units[unit]
-            z = ring.tile([P, HALF], F32, name="z", bufs=GATES)
             keep_gate = ring.tile([P, HALF], F32, name="keep_gate", bufs=GATES)
             cand = ring.tile([P, HALF], F32, name="cand", bufs=GATES)
             nc.scalar.activation(keep_gate[:], pair[0][:], ACT.Sigmoid, bias=signed_bz[:, c : c + 1], scale=-1.0)
-            nc.scalar.activation(z[:], pair[0][:], ACT.Sigmoid, bias=signed_bz[:, TILES + c : TILES + c + 1])
-            nc.scalar.activation(cand[:], pair[1][:], ACT.Tanh, bias=bn_cols[:, c : c + 1])
-            kept = ring.tile([P, HALF], F32, name="kept", bufs=TERMS)
+            nc.scalar.activation(cand[:], pair[1][:], ACT.Tanh, bias=neg_bn[:, c : c + 1], scale=-1.0)
+            if unit == 2:
+                kept = staging([P, HALF], F32, "kept", 1)
+            else:
+                kept = ring.tile([P, HALF], F32, name="kept", bufs=TERMS)
             nc.vector.tensor_tensor(kept[:], h_tiles[c][:].indirect(listed(h)), keep_gate[:], ALU.mult)
             new = ring.tile([P, HALF], F32, name="new", bufs=TERMS)
-            nc.vector.tensor_tensor(new[:], z[:], cand[:], ALU.mult)
+            nc.vector.scalar_tensor_tensor(new[:], keep_gate[:], 1.0, cand[:], ALU.subtract, ALU.mult)
             return kept, new
 
         blocks = [slice(b * P, (b + 1) * P) for b in range(HALF // P)]
@@ -300,22 +315,24 @@ def tile_list_tgn_ema_kernel(
         load_vector(bias_rows, BN_ROW, bn)
         load_w(0, 0)
         load_u(0, 0, CHUNK)
-        load_scales(u_sc[0], uz_scales)
+        load_scales(u_sc_first[0], uz_scales, slice(0, CHUNK // 4))
         gather_words(0, "first_words")
         gather_words(1, "second_words")
         gather_scales(0, ["first_scales0", "first_scales1"])
         load_u(1, 0, CHUNK)
         load_w(0, 1)
-        load_scales(u_sc[1], un_scales)
+        load_scales(u_sc_first[1], un_scales, slice(0, CHUNK // 4))
         load_vector(wgo_rows, 0, wgo[0, :])
         load_h(0)
-        load_h(1)
         x_late = [load_x(a, 1) for a in range(PASSES)]
+        load_h(1)
         for g in range(2):
             load_w(1, g)
-        for g in range(2):
-            load_u(g, CHUNK, CHUNK)
+        load_u(0, CHUNK, CHUNK)
+        load_scales(u_sc_rest[0], uz_scales, slice(CHUNK // 4, N // 4))
         load_h(2)
+        load_u(1, CHUNK, CHUNK)
+        load_scales(u_sc_rest[1], un_scales, slice(CHUNK // 4, N // 4))
         prep_x(0, 0, x_early[0])
         prep_x(1, 0, x_early[1])
         turn_biases()
@@ -339,20 +356,19 @@ def tile_list_tgn_ema_kernel(
         def ahead(step):
             if step == 1:
                 prep_x(0, 1, x_late[0])
-                prep_x(1, 1, x_late[1], step, (nc.scalar.copy, nc.vector.tensor_copy))
+                prep_x(1, 1, x_late[1], step)
             if step == 2:
                 prep_w(2, 0)
                 prep_w(2, 1, step)
                 load_h(3)
-                for g in range(2):
-                    load_w(2, g)
+                load_late_z()
+                load_w(2, 1)
                 for g in range(2):
                     load_u(g, 2 * CHUNK, 2 * CHUNK)
             if step == 3:
                 load_h(4)
                 load_h(5)
-                for g in range(2):
-                    load_w(3, g)
+                load_w(3, 1)
             c, g = divmod(step + 3, 2)
             if 3 <= c < last_tiles[-1] and (c not in ratio_tiles or g == 1):
                 prep_w(c, g)
@@ -384,6 +400,14 @@ def tile_list_tgn_ema_kernel(
             if step - 2 in ratio_tiles:
                 for h in range(2):
                     hold_argument(units.index((step - 2, h)), pair_of(step + 2)[h])
+            if step < DIRECT:
+                scatter(step, add_direct(step, *parts[step]))
+            if step - 2 >= DIRECT:
+                total = turn_back(turned[step - 2], pair[0])
+            if DIRECT <= step - 1 < len(units):
+                turned[step - 1] = add_turned(step - 1, *parts[step - 1], pair[1])
+            if step - 2 >= DIRECT:
+                scatter(step - 2, total)
             if step == FIRST_RATIO - 1:
                 floor = floor_column("floor", FLOOR)
             if step in (FIRST_RATIO - 1, FIRST_RATIO):
@@ -393,11 +417,3 @@ def tile_list_tgn_ema_kernel(
                     nc.scalar.activation(ratio(unit), held(unit), ACT.Exp, bias=floor, scale=-1.0)
             if step == FIRST_RATIO:
                 neg_floor = floor_column("neg_floor", -FLOOR)
-            if step < DIRECT:
-                scatter(step, add_direct(step, *parts[step]))
-            if step - 2 >= DIRECT:
-                total = turn_back(turned[step - 2], pair[0])
-            if DIRECT <= step - 1 < len(units):
-                turned[step - 1] = add_turned(step - 1, *parts[step - 1], pair[1])
-            if step - 2 >= DIRECT:
-                scatter(step - 2, total)

@@ -59,9 +59,6 @@ def tile_list_tgn_ema_kernel(
         u_sc_rest = [keep.tile([P, PASSES, (N - CHUNK) // 4], I32, name=f"u_sc_rest{g}", align_bytes=64) for g in range(2)]
         for sc_tile in [tab_sc] + u_sc_first + u_sc_rest:
             nc.vector.memset(sc_tile[:], 0)
-        warm = keep.tile([P, 8], F32, name="warm")
-        nc.vector.memset(warm[:, 0:4], 0.0)
-        nc.scalar.activation(warm[:, 4:8], warm[:, 0:4], ACT.Sigmoid)
 
         bias_rows = keep.tile([P, P], F32, name="bias_rows")
         nc.vector.memset(bias_rows[:], 0.0)

from contextlib import ExitStack

import concourse.mybir as mybir
from concourse.masks import make_identity

K, M, N, T, J = 1024, 1024, 1024, 2048, 1024
FLOPS = 2 * 2 * (K + M) * N * J

F32 = mybir.dt.float32
BF16 = mybir.dt.bfloat16
I32 = mybir.dt.int32
U32 = mybir.dt.uint32
U16 = mybir.dt.uint16
U8 = mybir.dt.uint8
FP8X4 = mybir.dt.float8_e4m3fn_x4
FP4X4 = mybir.dt.float4_e2m1fn_x4
ACT = mybir.ActivationFunctionType
ALU = mybir.AluOpType

P = 128
PACK = 4
KP = P * PACK
PASSES = 2
HALF = 512
QUARTER = 256
CHUNK = 256
TILES = N // P
WINDOWS = 3
RAW = 5
WIDE = 4
DIRECT = 3
FIRST_RATIO = 10
FLOOR = 24.0
PARKED = 4
BN_ROW = 32
GROUPED = 4
GATES = 3
TERMS = 4


def tile_list_tgn_ema_kernel(
    tc, x, tab_words, tab_scales, wz, uz_words, uz_scales, wn, un_words, un_scales, bz, bn, hT, wgo, offs, out
):
    nc = tc.nc
    with ExitStack() as ctx:
        keep = ctx.enter_context(tc.tile_pool(name="keep", bufs=1))
        ring = ctx.enter_context(tc.tile_pool(name="ring", bufs=2))
        psum = ctx.enter_context(tc.psum_pool(name="psum", bufs=1))
        banks = [psum.tile([P, HALF], F32, name=f"bank{b}") for b in range(8)]

        offsets = keep.tile([P, J // 16], U16, name="offsets")
        nc.sync.dma_start(offsets[:], offs)

        def listed(h):
            return offsets[:, h * HALF // 16 : (h + 1) * HALF // 16]

        tab_sc = keep.tile([P, PASSES, T // 4], I32, name="tab_sc", align_bytes=64)
        u_sc_first = [keep.tile([P, PASSES, CHUNK // 4], I32, name=f"u_sc_first{g}", align_bytes=64) for g in range(2)]
        u_sc_rest = [keep.tile([P, PASSES, (N - CHUNK) // 4], I32, name=f"u_sc_rest{g}", align_bytes=64) for g in range(2)]
        for sc_tile in [tab_sc] + u_sc_first + u_sc_rest:
            nc.vector.memset(sc_tile[:], 0)

        bias_rows = keep.tile([P, P], F32, name="bias_rows")
        nc.vector.memset(bias_rows[:], 0.0)
        wgo_rows = keep.tile([P, P], F32, name="wgo_rows")
        nc.vector.memset(wgo_rows[:], 0.0)
        wgo_cols = keep.tile([P, J // P], F32, name="wgo_cols")
        ident = keep.tile([P, P], F32, name="ident")
        make_identity(nc, ident[:])
        tab_w = ring.tile([P, T], I32, name="tab_w", tag="wide", bufs=WIDE)
        bn_cols = keep.tile([P, TILES], F32, name="bn_cols")
        signed_bz = keep.tile([P, TILES], F32, name="signed_bz", tag="gate_bias")
        neg_bn = keep.tile([P, TILES], F32, name="neg_bn")
        raised_bz = keep.tile([P, TILES], F32, name="raised_bz")
        wgo_sb = keep.tile([P, J], F32, name="wgo_sb")

        def load_vector(rows, row, vector):
            nc.sync.dma_start(out=rows[row : row + TILES, :], in_=vector.rearrange("(c p) -> c p", p=P))

        def load_scales(sc_tile, scales, words=slice(None)):
            for quad in range(4):
                rows = scales.bitcast(I32)[:, 4 * quad : 4 * quad + 4, words]
                nc.sync.dma_start(out=sc_tile[32 * quad : 32 * quad + 4, :, :], in_=rows.rearrange("a r n -> r a n"))

        def turn_biases():
            nc.tensor.transpose(banks[7][:, 0:P], bias_rows[:], ident[:])
            nc.scalar.copy(bn_cols[:], banks[7][:, BN_ROW : BN_ROW + TILES])
            nc.scalar.activation(signed_bz[:, 0:TILES], banks[7][:, 0:TILES], ACT.Copy, scale=-1.0)
            nc.scalar.activation(neg_bn[:], banks[7][:, BN_ROW : BN_ROW + TILES], ACT.Copy, scale=-1.0)
            nc.scalar.activation(raised_bz[:], banks[7][:, 0:TILES], ACT.Copy, bias=FLOOR)

        def spread_event_weights():
            nc.tensor.transpose(banks[4][:, 0:P], wgo_rows[:], ident[:])
            nc.scalar.copy(wgo_cols[:], banks[4][:, 0 : J // P])
            for h in range(2):
                for b in range(HALF // P):
                    col = h * (HALF // P) + b
                    nc.tensor.transpose(
                        banks[5 + h][:, b * P : (b + 1) * P], wgo_cols[:, col : col + 1].to_broadcast([P, P]), ident[:]
                    )
                nc.scalar.copy(wgo_sb[:, h * HALF : (h + 1) * HALF], banks[5 + h][:])

        windows = [keep.tile([P, T], F32, name=f"window{b}") for b in range(WINDOWS)]

        def staging(shape, dtype, name, shared):
            if shared is None:
                return ring.tile(shape, dtype, name=name, tag="grouped", bufs=GROUPED, align_bytes=64)
            return ring.tile(shape, dtype, name=name, tag=f"shared{shared}", bufs=1, align_bytes=64)

        v_codes, v_sc = {}, {}

        def gather_words(h, shared):
            pairs = staging([P, HALF], U32, "v_pairs", shared)
            nc.vector.tensor_copy(pairs[:], tab_w[:].bitcast(U32).indirect(listed(h)))
            v_codes[h] = keep.tile([P, PASSES * 2 * HALF], U8, name=f"v_codes{h}", align_bytes=64)
            nc.vector.tensor_copy(
                v_codes[h][:].bitcast(U16).rearrange("p (a j) -> p a j", a=PASSES),
                pairs[:].bitcast(U16).rearrange("p (j a) -> p a j", a=PASSES),
            )

        def gather_scales(h, shared):
            for a in range(PASSES):
                v_sc[h, a] = staging([P, HALF], U8, "v_sc", shared[a])
                nc.vector.tensor_copy(v_sc[h, a][:], tab_sc[:, a, :].bitcast(U8).indirect(listed(h)))

        def load_rows(raw, rows):
            nc.sync.dma_start(out=raw, in_=rows.rearrange("(p i) w -> p i w", i=PACK))

        def interleave(grouped, raw, copy):
            copy(out=grouped.rearrange("p (c e) i -> p c i e", e=4), in_=raw.rearrange("p i (c e) -> p c i e", e=4))

        x_codes = keep.tile([P, PASSES, J], U32, name="x_codes", align_bytes=64)
        x_sc = keep.tile([P, PASSES, J], U8, name="x_sc", align_bytes=64)

        def load_x(a, h):
            raw = ring.tile([P, PACK, HALF], F32, name="x_raw", tag="raw", bufs=RAW)
            load_rows(raw[:], x[a * KP : (a + 1) * KP, h * HALF : (h + 1) * HALF])
            return raw

        def prep_x(a, h, raw, shared=None):
            for s0 in range(0, HALF, QUARTER):
                grouped = staging([P, QUARTER, PACK], BF16, "x_grouped", shared if s0 + QUARTER == HALF else None)
                interleave(grouped[:], raw[:, :, s0 : s0 + QUARTER], nc.scalar.copy)
                cols = slice(h * HALF + s0, h * HALF + s0 + QUARTER)
                nc.vector.quantize_mx(
                    out=x_codes[:, a, cols].bitcast(FP8X4), scales=x_sc[:, a, cols], in_=grouped[:].rearrange("p w i -> p (w i)")
                )

        w_dram = (wz, wn)
        u_dram = (uz_words, un_words)
        u_codes = [keep.tile([P, PASSES, N], I32, name=f"u_codes{g}", align_bytes=64) for g in range(2)]
        w_raw, w_codes, w_sc = {}, {}, {}

        def load_w(ch, g):
            raw = ring.tile([P, PASSES, PACK, CHUNK], F32, name="w_raw", tag="raw", bufs=RAW)
            for a in range(PASSES):
                load_rows(raw[:, a, :, :], w_dram[g][a * KP : (a + 1) * KP, ch * CHUNK : (ch + 1) * CHUNK])
            for t in range(CHUNK // P):
                w_raw[ch * CHUNK // P + t, g] = [raw[:, a, :, t * P : (t + 1) * P] for a in range(PASSES)]

        def load_late_z():
            first = N - 2 * CHUNK
            raws = [ring.tile([P, PACK, 2 * CHUNK], F32, name="w_raw", tag="raw", bufs=RAW) for a in range(PASSES)]
            for a in range(PASSES):
                load_rows(raws[a][:], wz[a * KP : (a + 1) * KP, first:N])
            for t in range(2 * CHUNK // P):
                w_raw[first // P + t, 0] = [raw[:, :, t * P : (t + 1) * P] for raw in raws]

        def load_u(g, n0, width):
            words = u_dram[g].rearrange("a p n i -> p a (n i)")[:, :, 4 * n0 : 4 * (n0 + width)].bitcast(I32)
            nc.sync.dma_start(out=u_codes[g][:, :, n0 : n0 + width], in_=words)

        def prep_w(c, g, shared=None, copy=nc.scalar.copy):
            grouped = staging([P, PASSES, P, PACK], BF16, "w_grouped", shared)
            for a in range(PASSES):
                interleave(grouped[:, a, :, :], w_raw[c, g][a], copy)
            codes = keep.tile([P, PASSES * P], U32, name=f"w_codes{c}_{g}", align_bytes=64)
            sc = keep.tile([P, PASSES * P], U8, name=f"w_sc{c}_{g}", align_bytes=64)
            nc.vector.quantize_mx(
                out=codes[:].bitcast(FP8X4), scales=sc[:], in_=grouped[:].rearrange("p a w i -> p (a w i)")
            )
            w_codes[c, g], w_sc[c, g] = codes, sc

        h_tiles = {}

        def load_h(c):
            h_tiles[c] = ring.tile([P, T], F32, name="h_tile", tag="wide", bufs=WIDE)
            nc.sync.dma_start(out=h_tiles[c][:], in_=hT[c * P : (c + 1) * P, :])

        def multiply(c, h, gate_banks):
            cols = slice(c * P, (c + 1) * P)
            events = slice(h * HALF, (h + 1) * HALF)
            if cols.stop <= CHUNK:
                u_sc, sc_cols = u_sc_first, cols
            else:
                u_sc, sc_cols = u_sc_rest, slice(cols.start - CHUNK, cols.stop - CHUNK)
            for g, bank in gate_banks:
                for a in range(PASSES):
                    nc.tensor.matmul_mx(
                        out=bank[:],
                        lhsT=u_codes[g][:, a, cols].bitcast(FP8X4),
                        lhsT_scale=u_sc[g][:, a, :].bitcast(U8)[:, sc_cols],
                        rhs=v_codes[h][:, a * 2 * HALF : (a + 1) * 2 * HALF].bitcast(FP4X4),
                        rhs_scale=v_sc[h, a][:],
                        start=(a == 0),
                        stop=False,
                    )
                for a in range(PASSES):
                    nc.tensor.matmul_mx(
                        out=bank[:],
                        lhsT=w_codes[c, g][:, a * P : (a + 1) * P].bitcast(FP8X4),
                        lhsT_scale=w_sc[c, g][:, a * P : (a + 1) * P],
                        rhs=x_codes[:, a, events].bitcast(FP8X4),
                        rhs_scale=x_sc[:, a, events],
                        start=False,
                        stop=(a == PASSES - 1),
                    )

        parked = []

        def parked_part(kind, unit):
            if not parked:
                parked.extend(ring.tile([P, PARKED * HALF], F32, name="parked", tag="raw", bufs=RAW) for b in range(3))
            n = unit - FIRST_RATIO
            tile, at = (parked[kind], n) if n < PARKED else (parked[2], 2 * kind + n - PARKED)
            return tile[:, at * HALF : (at + 1) * HALF]

        def held(unit):
            return parked_part(0, unit)

        def ratio(unit):
            return parked_part(1, unit)

        def late_z(unit):
            return ratio(unit + 1 if unit + 1 < len(units) else FIRST_RATIO)

        def hold_argument(unit, bank):
            c, h = units[unit]
            multiply(c, h, [(0, bank)])
            nc.scalar.activation(held(unit), bank[:], ACT.Relu, bias=raised_bz[:, c : c + 1])

        def floor_column(name, value):
            column = keep.tile([P, TILES], F32, name=name, tag="gate_bias")
            nc.scalar.activation(column[:], raised_bz[:], ACT.Copy, scale=0.0, bias=value)
            return column[:, 0:1]

        def gate_ratio(unit, pair):
            c, h = units[unit]
            cand = ring.tile([P, HALF], F32, name="cand", bufs=GATES)
            nc.scalar.activation(cand[:], pair[1][:], ACT.Tanh, bias=bn_cols[:, c : c + 1])
            kept = ring.tile([P, HALF], F32, name="kept", bufs=TERMS)
            nc.vector.tensor_tensor(kept[:], h_tiles[c][:].indirect(listed(h)), ratio(unit), ALU.mult)
            return kept, cand

        def gate_product(unit, pair):
            c, h = units[unit]
            keep_gate = ring.tile([P, HALF], F32, name="keep_gate", bufs=GATES)
            cand = ring.tile([P, HALF], F32, name="cand", bufs=GATES)
            nc.scalar.activation(keep_gate[:], pair[0][:], ACT.Sigmoid, bias=signed_bz[:, c : c + 1], scale=-1.0)
            nc.scalar.activation(cand[:], pair[1][:], ACT.Tanh, bias=neg_bn[:, c : c + 1], scale=-1.0)
            if unit == 2:
                kept = staging([P, HALF], F32, "kept", 1)
            else:
                kept = ring.tile([P, HALF], F32, name="kept", bufs=TERMS)
            nc.vector.tensor_tensor(kept[:], h_tiles[c][:].indirect(listed(h)), keep_gate[:], ALU.mult)
            new = ring.tile([P, HALF], F32, name="new", bufs=TERMS)
            nc.vector.scalar_tensor_tensor(new[:], keep_gate[:], 1.0, cand[:], ALU.subtract, ALU.mult)
            return kept, new

        blocks = [slice(b * P, (b + 1) * P) for b in range(HALF // P)]

        def add_direct(step, kept, new):
            if step > 0:
                total = staging([P, HALF], F32, "total", step)
            else:
                total = ring.tile([P, HALF], F32, name="total", bufs=GATES)
            nc.vector.tensor_tensor(total[:], new[:], kept[:], ALU.add)
            return total

        def add_turned(unit, kept, new, bank):
            for blk in blocks:
                nc.tensor.matmul(bank[:, blk], kept[:, blk], ident[:], start=True, stop=False, is_transpose=True)
                nc.tensor.matmul(bank[:, blk], new[:, blk], ident[:], start=False, stop=True, is_transpose=True)
            by_event = ring.tile([P, HALF], F32, name="by_event", bufs=GATES)
            if unit < FIRST_RATIO:
                nc.scalar.copy(by_event[:], bank[:])
            else:
                for b, blk in enumerate(blocks):
                    col = units[unit][1] * len(blocks) + b
                    nc.scalar.activation(by_event[:, blk], bank[:, blk], ACT.Copy, scale=wgo_cols[:, col : col + 1])
            return by_event

        def turn_back(by_event, bank):
            for blk in blocks:
                nc.tensor.transpose(bank[:, blk], by_event[:, blk], ident[:])
            total = ring.tile([P, HALF], F32, name="total", bufs=GATES)
            nc.scalar.copy(total[:], bank[:])
            return total

        def scatter(unit, total):
            c, h = units[unit]
            window = windows[c % WINDOWS]
            factor = wgo_sb[:, h * HALF : (h + 1) * HALF] if unit < FIRST_RATIO else late_z(unit)
            nc.vector.tensor_tensor(window[:].indirect(listed(h)), total[:], factor, ALU.mult)
            if h == 1:
                nc.sync.dma_start(out=out[c * P : (c + 1) * P, :], in_=window[:])

        nc.sync.dma_start(out=tab_w[:], in_=tab_words[0].rearrange("p t b -> p (t b)").bitcast(I32))
        load_scales(tab_sc, tab_scales)
        x_early = [load_x(a, 0) for a in range(PASSES)]
        load_vector(bias_rows, 0, bz)
        load_vector(bias_rows, BN_ROW, bn)
        load_w(0, 0)
        load_u(0, 0, CHUNK)
        load_scales(u_sc_first[0], uz_scales, slice(0, CHUNK // 4))
        gather_words(0, "first_words")
        gather_words(1, "second_words")
        gather_scales(0, ["first_scales0", "first_scales1"])
        load_u(1, 0, CHUNK)
        load_w(0, 1)
        load_scales(u_sc_first[1], un_scales, slice(0, CHUNK // 4))
        load_vector(wgo_rows, 0, wgo[0, :])
        load_h(0)
        x_late = [load_x(a, 1) for a in range(PASSES)]
        load_h(1)
        for g in range(2):
            load_w(1, g)
        load_u(0, CHUNK, CHUNK)
        load_scales(u_sc_rest[0], uz_scales, slice(CHUNK // 4, N // 4))
        load_h(2)
        load_u(1, CHUNK, CHUNK)
        load_scales(u_sc_rest[1], un_scales, slice(CHUNK // 4, N // 4))
        prep_x(0, 0, x_early[0])
        prep_x(1, 0, x_early[1])
        turn_biases()
        prep_w(0, 0, "z0")
        prep_w(1, 0, "z1")
        prep_w(0, 1, None, nc.vector.tensor_copy)
        spread_event_weights()
        prep_w(1, 1)
        gather_scales(1, ["z0", "z1"])
        for window in windows:
            nc.vector.memset(window[:], 0.0)

        first_tiles, last_tiles = range(2), range(TILES - 2, TILES)
        units = [(c, h) for h in range(2) for c in first_tiles]
        units = units + [(c, h) for c in range(2, TILES - 2) for h in range(2)]
        units = units + [(c, h) for h in range(2) for c in last_tiles]

        ratio_tiles = range(FIRST_RATIO // 2, TILES)
        ratio_units = range(FIRST_RATIO, len(units))

        def ahead(step):
            if step == 1:
                prep_x(0, 1, x_late[0])
                prep_x(1, 1, x_late[1], step)
            if step == 2:
                prep_w(2, 0)
                prep_w(2, 1, step)
                load_h(3)
                load_late_z()
                load_w(2, 1)
                for g in range(2):
                    load_u(g, 2 * CHUNK, 2 * CHUNK)
            if step == 3:
                load_h(4)
                load_h(5)
                load_w(3, 1)
            c, g = divmod(step + 3, 2)
            if 3 <= c < last_tiles[-1] and (c not in ratio_tiles or g == 1):
                prep_w(c, g)
            if step == 2 * last_tiles[-1] - 3:
                prep_w(last_tiles[-1], 1)
            if step in ratio_tiles:
                prep_w(step, 0)
            if step in (5, 7):
                load_h(step // 2 + WIDE)

        def pair_of(step):
            return banks[2 * (step % 4) : 2 * (step % 4) + 2]

        parts, turned = {}, {}
        multiply(*units[0], enumerate(pair_of(0)))
        for step in range(len(units) + 2):
            pair = pair_of(step)
            if step < FIRST_RATIO:
                parts[step] = gate_product(step, pair)
            elif step < len(units):
                parts[step] = gate_ratio(step, pair)
            if step - 1 in ratio_units:
                nc.scalar.activation(late_z(step - 1), held(step - 1), ACT.Sigmoid, bias=neg_floor)
            ahead(step)
            if step + 1 < FIRST_RATIO:
                multiply(*units[step + 1], enumerate(pair_of(step + 1)))
            elif step + 1 < len(units):
                multiply(*units[step + 1], [(1, pair_of(step + 1)[1])])
            if step - 2 in ratio_tiles:
                for h in range(2):
                    hold_argument(units.index((step - 2, h)), pair_of(step + 2)[h])
            if step < DIRECT:
                scatter(step, add_direct(step, *parts[step]))
            if step - 2 >= DIRECT:
                total = turn_back(turned[step - 2], pair[0])
            if DIRECT <= step - 1 < len(units):
                turned[step - 1] = add_turned(step - 1, *parts[step - 1], pair[1])
            if step - 2 >= DIRECT:
                scatter(step - 2, total)
            if step == FIRST_RATIO - 1:
                floor = floor_column("floor", FLOOR)
            if step in (FIRST_RATIO - 1, FIRST_RATIO):
                share = len(ratio_units) // 2
                first = (step - FIRST_RATIO + 1) * share
                for unit in ratio_units[first : first + share]:
                    nc.scalar.activation(ratio(unit), held(unit), ACT.Exp, bias=floor, scale=-1.0)
            if step == FIRST_RATIO:
                neg_floor = floor_column("neg_floor", -FLOOR)
